import numpy as np
import ml_dtypes


def mxq(x, axis, fmt="e4m3"):
    dtype, down = {"e4m3": (ml_dtypes.float8_e4m3fn, 7), "e5m2": (ml_dtypes.float8_e5m2, 14)}[fmt]
    v = np.moveaxis(np.asarray(x, np.float32).astype(ml_dtypes.bfloat16).astype(np.float64), axis, -1)
    blocks = v.reshape(v.shape[:-1] + (-1, 32))
    amax = np.abs(blocks).max(-1, keepdims=True)
    byte = np.maximum(np.where(amax > 0, np.frexp(amax)[1] - 1 + 127, 0) - down, 1)
    scale = np.exp2(byte - 127.0)
    codes = (blocks / scale).astype(np.float32).astype(dtype).astype(np.float64)
    return np.moveaxis((codes * scale).reshape(v.shape), -1, axis)


WIDE = False


def mx_kscale(k):
    if not WIDE:
        return np.ones(k)
    levels = np.array([10, -10, 5, -5, 0])
    if k % 512:
        return np.exp2(np.random.permutation(np.resize(levels, k // 32))).repeat(32)
    a = np.empty((k // 512, 16))
    for p in range(k // 512):
        a[p, :8] = np.random.permutation(np.resize(levels, 8))
        for g in range(8):
            far = levels[np.abs(levels - a[p, g]) >= 10]
            a[p, g + 8] = far[np.random.randint(len(far))]
    return np.exp2(a.ravel()).repeat(32)


BF16 = ml_dtypes.bfloat16


def bf(x):
    return np.asarray(x, np.float32).astype(BF16)


def f64(x):
    return np.asarray(x).astype(np.float64)


E2M1 = np.array([0.0, 0.5, 1.0, 1.5, 2.0, 3.0, 4.0, 6.0, -0.0, -0.5, -1.0, -1.5, -2.0, -3.0, -4.0, -6.0])


def pack_weight(w, fmt):
    k, n = w.shape
    w = f64(bf(w)).reshape(k // 32, 32, n)
    amax = np.abs(w).max(1)
    if fmt == "e4m3":
        byte = np.frexp(amax)[1] - 1 + 127 - 7
    else:
        mant, ex = np.frexp(amax / 6.0)
        byte = np.where(mant > 0.5, ex, ex - 1) + 127
    byte = np.clip(np.where(amax > 0, byte, 1), 1, 254)
    scaled = (w * np.exp2(127.0 - byte)[:, None, :]).reshape(k, n).astype(np.float32)
    by_word = np.ascontiguousarray(scaled.reshape(k // 512, 128, 4, n).transpose(0, 1, 3, 2))
    if fmt == "e4m3":
        words = by_word.astype(ml_dtypes.float8_e4m3fn).view(np.uint8)
    else:
        c = by_word.astype(ml_dtypes.float4_e2m1fn).view(np.uint8) & 0xF
        words = c[..., 0::2] | (c[..., 1::2] << 4)
    return np.ascontiguousarray(words), np.ascontiguousarray(byte.astype(np.uint8).reshape(k // 512, 16, n))


def unpack_weight(words, scales, fmt):
    g, p, n, _ = words.shape
    if fmt == "e4m3":
        vals = np.ascontiguousarray(words).view(ml_dtypes.float8_e4m3fn).astype(np.float64)
    else:
        nib = np.empty((g, p, n, 4), np.uint8)
        nib[..., 0::2] = words & 0xF
        nib[..., 1::2] = words >> 4
        vals = E2M1[nib]
    vals = vals * np.repeat(np.exp2(scales.astype(np.float64) - 127.0), 8, axis=1)[..., None]
    return vals.transpose(0, 1, 3, 2).reshape(g * 512, n)
def pack4(w):
    words, scales = pack_weight(w, "e2m1")
    return words.reshape(words.shape[0], 128, -1), scales


def unpack4(words, scales):
    return unpack_weight(words.reshape(words.shape[0], 128, -1, 2), scales, "e2m1")


T, D, F, R = 1024, 1024, 1024, 512


def draw0():
    kd, kt = mx_kscale(D), mx_kscale(T)
    x = bf(np.random.standard_normal((T, D)) * kd)
    wm_words, wm_scales = pack4(np.random.standard_normal((D, F)) / np.sqrt(D) / kd[:, None])
    a_words, a_scales = pack4(np.random.standard_normal((D, R)) / np.sqrt(D) / kd[:, None])
    return {"x": x,
            "wm_words": wm_words,
            "wm_scales": wm_scales,
            "a_words": a_words,
            "a_scales": a_scales,
            "target": bf(np.random.standard_normal((T, F))),
            "s": bf((1.0 + 0.25 * np.random.standard_normal(T)) / kt),
            "wt": bf(np.random.uniform(0.5, 1.5, T) * kt)}


def scale_tokens(gain, rows):
    return gain[:, None] * rows


def core(x, wm_words, wm_scales, a_words, a_scales, target, s, wt):
    root_t = np.sqrt(T)
    xq = mxq(f64(x), 1, "e4m3")
    u = xq @ unpack4(a_words, a_scales)
    y = xq @ unpack4(wm_words, wm_scales)
    ug = scale_tokens(f64(s), u)
    e = scale_tokens(f64(wt), np.tanh(y - f64(target)))
    return (mxq(ug.T, 1, "e4m3") @ mxq(e, 0, "e4m3")) / root_t


def e4m3fn_bytes(y):
    return np.clip(np.asarray(y, np.float64), -448.0, 448.0).astype(np.float32).astype(ml_dtypes.float8_e4m3fn).view(np.uint8)


def e4m3fn_values(b):
    return np.asarray(b, np.uint8).view(ml_dtypes.float8_e4m3fn).astype(np.float64)


def setup_inputs():
    d = draw0()
    x0 = np.asarray(d['x']).astype(np.float64)
    s = (np.max(np.abs(x0), axis=(0,), keepdims=True) / 448.0).astype(np.float32)
    out = {}
    for k, v in d.items():
        if k == 'x':
            out['x_bytes'] = e4m3fn_bytes(x0 / s.astype(np.float64))
            out['x_scale'] = s
        else:
            out[k] = v
    return out


def reference(x_bytes, x_scale, wm_words, wm_scales, a_words, a_scales, target, s, wt):
    return core(e4m3fn_values(x_bytes) * x_scale.astype(np.float64), wm_words, wm_scales, a_words, a_scales, target, s, wt)

@@ -1,0 +1,487 @@
+from contextlib import ExitStack
+
+import concourse.mybir as mybir
+from concourse.masks import make_identity
+
+FLOPS = 2 * 1024 * 1024 * 512 * 2 + 2 * 1024 * 1024 * 1024
+
+P = 128
+T, D, F, R = 1024, 1024, 1024, 512
+F32 = mybir.dt.float32
+BF16 = mybir.dt.bfloat16
+I32 = mybir.dt.int32
+U32 = mybir.dt.uint32
+U8 = mybir.dt.uint8
+F8 = mybir.dt.float8_e4m3fn
+F8X4 = mybir.dt.float8_e4m3fn_x4
+F4X4 = mybir.dt.float4_e2m1fn_x4
+MULT = mybir.AluOpType.mult
+ADD = mybir.AluOpType.add
+SUB = mybir.AluOpType.subtract
+ACT = mybir.ActivationFunctionType
+WSPLIT = (0, 1,)
+O_WIDTH = {0: 512, 512: 256, 768: 128, 896: 128}
+
+ORDER = [
+    ("V", ("W", 0, 0), -1),
+    ("V", ("W", 0, 1), -1),
+    ("P", ("T", 0, 0), 0),
+    ("V", ("W", 1, 0), -1),
+    ("P", ("T", 0, 1), -1),
+    ("V", ("W", 1, 1), -1),
+    ("S", ("C", 0), -1),
+    ("P", ("T", 1, 0), 1),
+    ("P", ("T", 1, 1), -1),
+    ("V", ("Q", 0), -1),
+    ("S", ("C", 1), -1),
+    ("V", ("W", 2, 0), -1),
+    ("P", ("Y", 0, 512, 0), 2),
+    ("P", ("Y", 0, 0, 0), 3),
+    ("V", ("W", 3, 0), -1),
+    ("P", ("U", 0), 4),
+    ("P", ("T", 2, 0), 5),
+    ("V", ("Q", 1), -1),
+    ("S", ("G", 0), -1),
+    ("V", ("s", 0, 512, 0), -1),
+    ("P", ("T", 3, 0), 6),
+    ("S", ("C", 2), -1),
+    ("V", ("s", 0, 0, 0), -1),
+    ("P", ("Y", 0, 0, 1), 7),
+    ("S", ("th", 0, 512, 0), -1),
+    ("V", ("Q", 2), -1),
+    ("P", ("U", 1), 0),
+    ("S", ("C", 3), -1),
+    ("V", ("W", 4, 0), -1),
+    ("P", ("Y", 0, 512, 2), 1),
+    ("S", ("th", 0, 0, 0), -1),
+    ("P", ("Y", 0, 0, 2), 4),
+    ("S", ("G", 1), -1),
+    ("V", ("W", 6, 0), -1),
+    ("P", ("U", 2), 2),
+    ("P", ("Y", 0, 512, 1), 5),
+    ("V", ("W", 5, 0), -1),
+    ("S", ("G", 2), -1),
+    ("P", ("T", 4, 0), 3),
+    ("V", ("W", 7, 0), -1),
+    ("P", ("T", 6, 0), 6),
+    ("S", ("C", 4), -1),
+    ("P", ("T", 5, 0), 0),
+    ("S", ("C", 6), -1),
+    ("V", ("s", 0, 0, 2), -1),
+    ("P", ("T", 7, 0), 2),
+    ("S", ("C", 5), -1),
+    ("V", ("Q", 3), -1),
+    ("S", ("th", 0, 0, 2), -1),
+    ("V", ("s", 0, 0, 1), -1),
+    ("P", ("U", 3), 3),
+    ("S", ("C", 7), -1),
+    ("V", ("s", 0, 512, 2), -1),
+    ("P", ("Y", 0, 512, 3), 6),
+    ("S", ("th", 0, 0, 1), -1),
+    ("V", ("w", 0, 0, 2), -1),
+    ("V", ("Q", 7), -1),
+    ("P", ("Y", 0, 0, 3), 4),
+    ("S", ("G", 3), -1),
+    ("V", ("s", 0, 512, 3), -1),
+    ("P", ("U", 7), 0),
+    ("S", ("th", 0, 512, 2), -1),
+    ("V", ("s", 0, 0, 3), -1),
+    ("P", ("IU", 0, 0), 7),
+    ("S", ("th", 0, 512, 3), -1),
+    ("V", ("w", 0, 0, 1), -1),
+    ("V", ("Q", 6), -1),
+    ("P", ("Y", 1, 0, 3), 2),
+    ("S", ("G", 7), -1),
+    ("V", ("s", 0, 512, 1), -1),
+    ("P", ("Y", 1, 0, 2), 1),
+    ("S", ("th", 0, 0, 3), -1),
+    ("V", ("s", 1, 0, 3), -1),
+    ("P", ("IU", 0, 1), 3),
+    ("S", ("th", 0, 512, 1), -1),
+    ("V", ("Q", 5), -1),
+    ("P", ("U", 6), 6),
+    ("V", ("w", 0, 0, 3), -1),
+    ("S", ("th", 1, 0, 3), -1),
+    ("V", ("w", 0, 512, 3), -1),
+    ("P", ("U", 5), 4),
+    ("V", ("w", 0, 512, 1), -1),
+    ("S", ("G", 6), -1),
+    ("V", ("Q", 4), -1),
+    ("P", ("Y", 1, 0, 1), 0),
+    ("V", ("w", 1, 0, 3), -1),
+    ("S", ("G", 5), -1),
+    ("V", ("s", 1, 0, 2), -1),
+    ("P", ("Y", 1, 640), 5),
+    ("S", ("IUc", 0, 0), -1),
+    ("V", ("s", 1, 0, 1), -1),
+    ("P", ("Y", 1, 0, 0), 2),
+    ("S", ("th", 1, 0, 2), -1),
+    ("V", ("s", 1, 640), -1),
+    ("P", ("Y", 1, 896), 6),
+    ("S", ("th", 1, 0, 1), -1),
+    ("V", ("w", 0, 0, 0), -1),
+    ("V", ("w", 1, 0, 2), -1),
+    ("P", ("U", 4), 4),
+    ("S", ("th", 1, 640), -1),
+    ("V", ("s", 1, 896), -1),
+    ("P", ("I", 0, 0, 1), 1),
+    ("S", ("IUc", 0, 1), -1),
+    ("V", ("w", 1, 0, 1), -1),
+    ("P", ("Y", 1, 512), 7),
+    ("V", ("w", 0, 512, 0), -1),
+    ("S", ("G", 4), -1),
+    ("V", ("s", 1, 0, 0), -1),
+    ("P", ("Y", 1, 768), 0),
+    ("S", ("Ic", 0, 0, 1), -1),
+    ("V", ("QU", 0), -1),
+    ("P", ("IU", 1, 1), 5),
+    ("S", ("th", 1, 0, 0), -1),
+    ("V", ("s", 1, 512), -1),
+    ("P", ("IU", 1, 0), 6),
+    ("S", ("th", 1, 896), -1),
+    ("V", ("s", 1, 768), -1),
+    ("P", ("I", 0, 0, 0), 3),
+    ("S", ("IUc", 1, 1), -1),
+    ("V", ("w", 1, 0, 0), -1),
+    ("V", ("w", 1, 896), -1),
+    ("S", ("IUc", 1, 0), -1),
+    ("P", ("I", 1, 0, 1), 4),
+    ("V", ("w", 0, 512, 2), -1),
+    ("S", ("Ic", 0, 0, 0), -1),
+    ("P", ("I", 1, 0, 0), 2),
+    ("V", ("QE", 1, 896), -1),
+    ("V", ("QU", 1), -1),
+    ("S", ("Ic", 1, 0, 1), -1),
+    ("P", ("I", 0, 512, 1), 1),
+    ("V", ("QE", 0, 0), -1),
+    ("S", ("Ic", 1, 0, 0), -1),
+    ("P", ("I", 0, 512, 0), 7),
+    ("V", ("w", 1, 640), -1),
+    ("S", ("Ic", 0, 512, 1), -1),
+    ("P", ("O", 0, 2, 0), 0),
+    ("P", ("O", 0, 0, 0), 5),
+    ("V", ("QE", 1, 0), -1),
+    ("S", ("Ic", 0, 512, 0), -1),
+    ("P", ("O", 0, 3, 0), 6),
+    ("P", ("O", 0, 1, 0), 3),
+    ("V", ("QE", 1, 640), -1),
+    ("S", ("th", 1, 512), -1),
+    ("P", ("O", 0, 1, 1), -1),
+    ("V", ("QE", 0, 512), -1),
+    ("P", ("O", 0, 2, 1), -1),
+    ("S", ("th", 1, 768), -1),
+    ("P", ("O", 0, 3, 1), -1),
+    ("V", ("w", 1, 512), -1),
+    ("P", ("O", 0, 0, 1), -1),
+    ("S", ("Oc", 0, 2), -1),
+    ("P", ("O", 512, 0, 0), 4),
+    ("P", ("O", 512, 3, 0), 2),
+    ("V", ("w", 1, 768), -1),
+    ("P", ("O", 896, 0, 0), 1),
+    ("P", ("O", 768, 0, 0), 7),
+    ("S", ("Oc", 0, 0), -1),
+    ("P", ("O", 896, 0, 1), -1),
+    ("P", ("O", 512, 2, 0), 0),
+    ("V", ("QE", 1, 512), -1),
+    ("V", ("Oc", 0, 3), -1),
+    ("S", ("Oc", 896, 0), -1),
+    ("P", ("O", 512, 2, 1), -1),
+    ("P", ("O", 512, 0, 1), -1),
+    ("P", ("O", 768, 2, 0), 5),
+    ("V", ("QE", 1, 768), -1),
+    ("P", ("O", 512, 3, 1), -1),
+    ("S", ("Oc", 512, 2), -1),
+    ("P", ("O", 896, 3, 0), 1),
+    ("V", ("Oc", 0, 1), -1),
+    ("P", ("O", 896, 2, 0), 6),
+    ("S", ("Oc", 512, 0), -1),
+    ("P", ("O", 768, 2, 1), -1),
+    ("P", ("O", 768, 0, 1), -1),
+    ("P", ("O", 896, 3, 1), -1),
+    ("P", ("O", 512, 1, 0), 0),
+    ("S", ("Oc", 768, 2), -1),
+    ("V", ("Oc", 512, 3), -1),
+    ("P", ("O", 512, 1, 1), -1),
+    ("S", ("Oc", 768, 0), -1),
+    ("P", ("O", 768, 1, 0), 4),
+    ("P", ("O", 768, 1, 1), -1),
+    ("V", ("Oc", 896, 3), -1),
+    ("P", ("O", 896, 1, 0), 3),
+    ("P", ("O", 896, 1, 1), -1),
+    ("V", ("Oc", 512, 1), -1),
+    ("P", ("O", 896, 2, 1), -1),
+    ("P", ("O", 768, 3, 0), 5),
+    ("P", ("O", 768, 3, 1), -1),
+    ("V", ("Oc", 896, 1), -1),
+    ("S", ("Oc", 896, 2), -1),
+    ("V", ("Oc", 768, 1), -1),
+    ("V", ("Oc", 768, 3), -1),
+]
+
+
+def tile_lorafalogcoshgradient_w4_kernel(
+    tc, x_bytes, x_scale, wm_words, wm_scales, a_words, a_scales, target, s, wt, out
+):
+    nc = tc.nc
+    with ExitStack() as ctx:
+        keep = ctx.enter_context(tc.tile_pool(name="keep", bufs=1))
+        wide = ctx.enter_context(tc.tile_pool(name="wide", bufs=8))
+        zs = ctx.enter_context(tc.tile_pool(name="zs", bufs=10))
+        grp = ctx.enter_context(tc.tile_pool(name="grp", bufs=3))
+        outs = ctx.enter_context(tc.tile_pool(name="outs", bufs=6))
+        ps = ctx.enter_context(tc.psum_pool(name="ps", bufs=1))
+        ctx.enter_context(tc.manual_schedule())
+
+        warm = keep.tile([P, 1], F32)
+        nc.vector.memset(warm[:], 0.0)
+        nc.scalar.activation(out=warm[:], in_=warm[:], func=ACT.Tanh)
+        wm_sc = keep.tile([P, 2, F], U8, align_bytes=64)
+        a_sc = keep.tile([P, 2, R], U8, align_bytes=64)
+        nc.vector.memset(wm_sc[:].rearrange("p c n -> p (c n)").bitcast(I32), 0)
+        nc.vector.memset(a_sc[:].rearrange("p c n -> p (c n)").bitcast(I32), 0)
+        ident_f = keep.tile([P, P], F32)
+        make_identity(nc, ident_f[:])
+        ident_b = keep.tile([P, P], BF16)
+        make_identity(nc, ident_b[:])
+
+        xb_view = x_bytes.rearrange("(g p t) k -> g p t k", p=P, t=4)
+        tg_view = target.rearrange("(g p t) f -> g p t f", p=P, t=4)
+        xb = [keep.tile([P, D], U8, align_bytes=64, name=f"xb{i}") for i in range(8)]
+        tg = [keep.tile([P, 4, F], BF16, name=f"tg{i}") for i in range(2)]
+        xs = keep.tile([P, D], F32)
+        wm_w = keep.tile([P, 2, 2 * F], U8, align_bytes=64)
+        a_w = keep.tile([P, 2, 2 * R], U8, align_bytes=64)
+        s_b = keep.tile([P, 2, 4], BF16)
+        wt_b = keep.tile([P, 2, 4], BF16)
+        s_f = keep.tile([P, 2, 4], F32)
+        wt_f = keep.tile([P, 2, 4], F32)
+
+        def load_x(i):
+            nc.sync.dma_start(out=xb[i][:], in_=xb_view[i // 4, :, i % 4, :])
+
+        def load_t(i):
+            nc.sync.dma_start(out=tg[i // 4][:, i % 4, :], in_=tg_view[i // 4, :, i % 4, :])
+
+        def load_scales(dst, src):
+            for q in range(4):
+                nc.sync.dma_start(
+                    out=dst[32 * q : 32 * q + 4, :, :].bitcast(I32),
+                    in_=src[:, 4 * q : 4 * q + 4, :].rearrange("g q n -> q g n").bitcast(I32),
+                )
+
+        def load_xs(c):
+            nc.sync.dma_start(
+                out=xs[:, 512 * c : 512 * (c + 1)],
+                in_=x_scale[:, 512 * c : 512 * (c + 1)].rearrange("o k -> (o k)").partition_broadcast(P),
+            )
+
+        load_x(0)
+        load_xs(0)
+        load_xs(1)
+        load_x(1)
+        load_scales(wm_sc, wm_scales)
+        nc.sync.dma_start(out=wm_w[:, 0, :], in_=wm_words[0])
+        nc.sync.dma_start(out=wm_w[:, 1, :], in_=wm_words[1])
+        load_x(2)
+        load_x(3)
+        load_scales(a_sc, a_scales)
+        nc.sync.dma_start(out=s_b[:], in_=s.rearrange("(g p t) -> p g t", p=P, t=4))
+        nc.sync.dma_start(out=a_w[:, 0, :], in_=a_words[0])
+        nc.sync.dma_start(out=a_w[:, 1, :], in_=a_words[1])
+        for i in range(4):
+            load_t(i)
+        nc.sync.dma_start(out=wt_b[:], in_=wt.rearrange("(g p t) -> p g t", p=P, t=4))
+        for i in range(4, 8):
+            load_x(i)
+        for i in range(4, 8):
+            load_t(i)
+        nc.gpsimd.tensor_copy(out=s_f[:], in_=s_b[:])
+        nc.gpsimd.tensor_copy(out=wt_f[:], in_=wt_b[:])
+
+        x_codes = [keep.tile([P, 2 * P], U32, align_bytes=64, name=f"xc{i}") for i in range(8)]
+        x_sc = [keep.tile([P, 2 * P], U8, align_bytes=64, name=f"xsc{i}") for i in range(8)]
+        e_codes = [keep.tile([P, F], U32, align_bytes=64, name=f"ec{i}") for i in range(2)]
+        e_sc = [keep.tile([P, F], U8, align_bytes=64, name=f"esc{i}") for i in range(2)]
+        u_codes = [keep.tile([P, R], U32, align_bytes=64, name=f"uc{i}") for i in range(2)]
+        u_sc = [keep.tile([P, R], U8, align_bytes=64, name=f"usc{i}") for i in range(2)]
+        val = {}
+
+        def mm(dst, i, words, scales, lo, hi):
+            for c in range(2):
+                nc.tensor.matmul_mx(
+                    out=dst,
+                    lhsT=x_codes[i][:, P * c : P * (c + 1)].bitcast(F8X4),
+                    lhsT_scale=x_sc[i][:, P * c : P * (c + 1)],
+                    rhs=words[:, c, 2 * lo : 2 * hi].bitcast(F4X4),
+                    rhs_scale=scales[:, c, lo:hi],
+                    start=(c == 0),
+                    stop=(c == 1),
+                )
+
+        def interleave(dst, planar, h):
+            for j in range(2):
+                lo = 256 * h + 128 * j
+                nc.tensor.matmul(
+                    out=dst[:, 512 * j : 512 * (j + 1)].rearrange("p (f t) -> p f t", t=4),
+                    lhsT=ident_b[:],
+                    rhs=planar[:, :, lo : lo + 128].rearrange("p t f -> p f t"),
+                    start=True,
+                    stop=True,
+                )
+
+        def run(eng, tok, b):
+            kind = tok[0]
+            if b >= 0:
+                if kind == "T":
+                    bank = ps.tile([P, 2, 2, P], F32, name=f"bank{b}")
+                    val["T", tok[1]] = bank
+                elif kind == "Y" and len(tok) == 3:
+                    bank = ps.tile([P, 4, P], F32, name=f"bank{b}")
+                elif kind in ("I", "IU"):
+                    bank = ps.tile([P, 1024], BF16, name=f"bank{b}")
+                else:
+                    bank = ps.tile([P, 512], F32, name=f"bank{b}")
+            if kind == "W":
+                i, c = tok[1], tok[2]
+                lo, hi = (512 * c, 512 * c + 512) if i in WSPLIT else (0, 1024)
+                if ("W", i) not in val:
+                    xw = wide.tile([P, D], BF16, align_bytes=64, name="xw")
+                    val["W", i] = xw
+                nc.vector.tensor_tensor(out=val["W", i][:, lo:hi], in0=xb[i][:, lo:hi].bitcast(F8), in1=xs[:, lo:hi], op=MULT)
+            elif kind == "T":
+                i = tok[1]
+                words = val["W", i][:].bitcast(F32)
+                for c in (tok[2],) if i in WSPLIT else (0, 1):
+                    for u in range(2):
+                        nc.tensor.transpose(val["T", i][:, c, u, :], words[:, 256 * c + u : 256 * (c + 1) : 2], ident_f[:])
+            elif kind == "C":
+                i = tok[1]
+                xt = wide.tile([P, D], BF16, align_bytes=64, name="xt")
+                val["C", i] = xt
+                nc.scalar.copy(
+                    out=xt[:].bitcast(F32).rearrange("p (c r u) -> p c r u", c=2, u=2),
+                    in_=val["T", i][:].rearrange("p c u r -> p c r u"),
+                )
+            elif kind == "Q":
+                i = tok[1]
+                nc.vector.quantize_mx(out=x_codes[i][:].bitcast(F8X4), scales=x_sc[i][:], in_=val["C", i][:])
+            elif kind == "U":
+                val[tok] = bank
+                mm(bank[:], tok[1], a_w, a_sc, 0, 512)
+            elif kind == "G":
+                i = tok[1]
+                g, t = divmod(i, 4)
+                if ("up", g) not in val:
+                    up = grp.tile([P, 4, 512], BF16, name="up")
+                    val["up", g] = up
+                nc.scalar.activation(out=val["up", g][:, t, :], in_=val["U", i][:], func=ACT.Copy, scale=s_f[:, g, t : t + 1])
+            elif kind == "IU":
+                val[tok] = bank
+                interleave(bank, val["up", tok[1]], tok[2])
+            elif kind == "IUc":
+                g, h = tok[1], tok[2]
+                if ("ui", g) not in val:
+                    ui = grp.tile([P, 2048], BF16, align_bytes=64, name="ui")
+                    val["ui", g] = ui
+                nc.scalar.copy(out=val["ui", g][:, 1024 * h : 1024 * (h + 1)], in_=val["IU", g, h][:])
+            elif kind == "QU":
+                g = tok[1]
+                nc.vector.quantize_mx(out=u_codes[g][:].bitcast(F8X4), scales=u_sc[g][:], in_=val["ui", g][:])
+            elif kind == "Y":
+                val[tok] = bank
+                g, f0 = tok[1], tok[2]
+                if len(tok) == 4:
+                    mm(bank[:], 4 * g + tok[3], wm_w, wm_sc, f0, f0 + 512)
+                else:
+                    for t in range(4):
+                        mm(bank[:, t, :], 4 * g + t, wm_w, wm_sc, f0, f0 + P)
+            elif kind == "s":
+                g, f0 = tok[1], tok[2]
+                z = zs.tile([P, 512], F32, name="z")
+                val[tok] = z
+                if len(tok) == 4:
+                    nc.vector.tensor_tensor(out=z[:], in0=val[("Y",) + tok[1:]][:], in1=tg[g][:, tok[3], f0 : f0 + 512], op=SUB)
+                else:
+                    nc.vector.tensor_tensor(
+                        out=z[:].rearrange("p (f t) -> p f t", t=4),
+                        in0=val[("Y",) + tok[1:]][:].rearrange("p t f -> p f t"),
+                        in1=tg[g][:, :, f0 : f0 + P].rearrange("p t f -> p f t"),
+                        op=SUB,
+                    )
+            elif kind == "th":
+                th = zs.tile([P, 512], F32, name="th")
+                val[tok] = th
+                nc.scalar.activation(out=th[:], in_=val[("s",) + tok[1:]][:], func=ACT.Tanh)
+            elif kind == "w":
+                g, f0 = tok[1], tok[2]
+                if len(tok) == 4:
+                    t = tok[3]
+                    if ("ep", g, f0) not in val:
+                        ep = grp.tile([P, 4, 512], BF16, name="ep")
+                        val["ep", g, f0] = ep
+                    dst = val["ep", g, f0][:, t, :]
+                    src = val[("th",) + tok[1:]][:]
+                    if eng == "V":
+                        nc.vector.tensor_scalar(out=dst, in0=src, scalar1=wt_f[:, g, t : t + 1], scalar2=None, op0=MULT)
+                    elif eng == "G":
+                        nc.gpsimd.tensor_scalar(out=dst, in0=src, scalar1=wt_f[:, g, t : t + 1], scalar2=0.0, op0=MULT, op1=ADD)
+                    else:
+                        nc.scalar.activation(out=dst, in_=src, func=ACT.Copy, scale=wt_f[:, g, t : t + 1])
+                else:
+                    ei = zs.tile([P, 512], BF16, align_bytes=64, name="ei")
+                    val[tok] = ei
+                    nc.vector.tensor_tensor(
+                        out=ei[:].rearrange("p (f t) -> p f t", t=4),
+                        in0=val[("th",) + tok[1:]][:].rearrange("p (f t) -> p f t", t=4),
+                        in1=wt_f[:, g, :].unsqueeze(1).to_broadcast([P, P, 4]),
+                        op=MULT,
+                    )
+            elif kind == "I":
+                val[tok] = bank
+                interleave(bank, val["ep", tok[1], tok[2]], tok[3])
+            elif kind == "Ic":
+                g, f0, h = tok[1:]
+                if ("ei", g, f0) not in val:
+                    eint = grp.tile([P, 2048], BF16, align_bytes=64, name="eint")
+                    val["ei", g, f0] = eint
+                dst = val["ei", g, f0][:, 1024 * h : 1024 * (h + 1)]
+                if eng == "V":
+                    nc.vector.tensor_copy(out=dst, in_=val["I", g, f0, h][:])
+                else:
+                    nc.scalar.copy(out=dst, in_=val["I", g, f0, h][:])
+            elif kind == "QE":
+                g, f0 = tok[1], tok[2]
+                if ("ei", g, f0) in val:
+                    src, n = val["ei", g, f0], 512
+                else:
+                    src, n = val[("w",) + tok[1:]], P
+                nc.vector.quantize_mx(
+                    out=e_codes[g][:, f0 : f0 + n].bitcast(F8X4), scales=e_sc[g][:, f0 : f0 + n], in_=src[:]
+                )
+            elif kind == "O":
+                f0, rt, g = tok[1:]
+                n = O_WIDTH[f0]
+                if g == 0:
+                    val["O", f0, rt] = bank
+                nc.tensor.matmul_mx(
+                    out=val["O", f0, rt][:, 0:n],
+                    lhsT=u_codes[g][:, P * rt : P * (rt + 1)].bitcast(F8X4),
+                    lhsT_scale=u_sc[g][:, P * rt : P * (rt + 1)],
+                    rhs=e_codes[g][:, f0 : f0 + n].bitcast(F8X4),
+                    rhs_scale=e_sc[g][:, f0 : f0 + n],
+                    start=(g == 0),
+                    stop=(g == 1),
+                )
+            elif kind == "Oc":
+                f0, rt = tok[1:]
+                n = O_WIDTH[f0]
+                res = outs.tile([P, 512], F32, name="res")
+                src = val["O", f0, rt][:, 0:n]
+                if eng == "S":
+                    nc.scalar.activation(out=res[:, 0:n], in_=src, func=ACT.Copy, scale=1.0 / 32.0)
+                else:
+                    nc.vector.tensor_scalar(out=res[:, 0:n], in0=src, scalar1=1.0 / 32.0, scalar2=None, op0=MULT)
+                nc.sync.dma_start(out=out[P * rt : P * (rt + 1), f0 : f0 + n], in_=res[:, 0:n])
+
+        for eng, tok, b in ORDER:
+            run(eng, tok, b)

@@ -6,7 +6,7 @@ from concourse.masks import make_identity
 FLOPS = 2 * 1024 * 1024 * 512 * 2 + 2 * 1024 * 1024 * 1024
 
 P = 128
-T, D, F, R = 1024, 1024, 1024, 512
+D, F, R = 1024, 1024, 512
 F32 = mybir.dt.float32
 BF16 = mybir.dt.bfloat16
 I32 = mybir.dt.int32
@@ -16,206 +16,172 @@ F8 = mybir.dt.float8_e4m3fn
 F8X4 = mybir.dt.float8_e4m3fn_x4
 F4X4 = mybir.dt.float4_e2m1fn_x4
 MULT = mybir.AluOpType.mult
-ADD = mybir.AluOpType.add
 SUB = mybir.AluOpType.subtract
 ACT = mybir.ActivationFunctionType
-WSPLIT = (0, 1,)
-O_WIDTH = {0: 512, 512: 256, 768: 128, 896: 128}
+QE_SPAN = {(0, 0): 4, (0, 4): 4, (1, 0): 4, (1, 4): 2, (1, 6): 2}
+O_SPAN = {0: 4, 4: 2, 6: 2}
+O_POOL = {0: "TTBB", 4: "YYYY", 6: "TTBB"}
 
 ORDER = [
-    ("V", ("W", 0, 0), -1),
-    ("V", ("W", 0, 1), -1),
-    ("P", ("T", 0, 0), 0),
-    ("V", ("W", 1, 0), -1),
-    ("P", ("T", 0, 1), -1),
-    ("V", ("W", 1, 1), -1),
-    ("S", ("C", 0), -1),
-    ("P", ("T", 1, 0), 1),
-    ("P", ("T", 1, 1), -1),
-    ("V", ("Q", 0), -1),
-    ("S", ("C", 1), -1),
-    ("V", ("W", 2, 0), -1),
-    ("P", ("Y", 0, 512, 0), 2),
-    ("P", ("Y", 0, 0, 0), 3),
-    ("V", ("W", 3, 0), -1),
-    ("P", ("U", 0), 4),
-    ("P", ("T", 2, 0), 5),
-    ("V", ("Q", 1), -1),
-    ("S", ("G", 0), -1),
-    ("V", ("s", 0, 512, 0), -1),
-    ("P", ("T", 3, 0), 6),
-    ("S", ("C", 2), -1),
-    ("V", ("s", 0, 0, 0), -1),
-    ("P", ("Y", 0, 0, 1), 7),
-    ("S", ("th", 0, 512, 0), -1),
-    ("V", ("Q", 2), -1),
-    ("P", ("U", 1), 0),
-    ("S", ("C", 3), -1),
-    ("V", ("W", 4, 0), -1),
-    ("P", ("Y", 0, 512, 2), 1),
-    ("S", ("th", 0, 0, 0), -1),
-    ("P", ("Y", 0, 0, 2), 4),
-    ("S", ("G", 1), -1),
-    ("V", ("W", 6, 0), -1),
-    ("P", ("U", 2), 2),
-    ("P", ("Y", 0, 512, 1), 5),
-    ("V", ("W", 5, 0), -1),
-    ("S", ("G", 2), -1),
-    ("P", ("T", 4, 0), 3),
-    ("V", ("W", 7, 0), -1),
-    ("P", ("T", 6, 0), 6),
-    ("S", ("C", 4), -1),
-    ("P", ("T", 5, 0), 0),
-    ("S", ("C", 6), -1),
-    ("V", ("s", 0, 0, 2), -1),
-    ("P", ("T", 7, 0), 2),
-    ("S", ("C", 5), -1),
-    ("V", ("Q", 3), -1),
-    ("S", ("th", 0, 0, 2), -1),
-    ("V", ("s", 0, 0, 1), -1),
-    ("P", ("U", 3), 3),
-    ("S", ("C", 7), -1),
-    ("V", ("s", 0, 512, 2), -1),
-    ("P", ("Y", 0, 512, 3), 6),
-    ("S", ("th", 0, 0, 1), -1),
-    ("V", ("w", 0, 0, 2), -1),
-    ("V", ("Q", 7), -1),
-    ("P", ("Y", 0, 0, 3), 4),
-    ("S", ("G", 3), -1),
-    ("V", ("s", 0, 512, 3), -1),
-    ("P", ("U", 7), 0),
-    ("S", ("th", 0, 512, 2), -1),
-    ("V", ("s", 0, 0, 3), -1),
-    ("P", ("IU", 0, 0), 7),
-    ("S", ("th", 0, 512, 3), -1),
-    ("V", ("w", 0, 0, 1), -1),
-    ("V", ("Q", 6), -1),
-    ("P", ("Y", 1, 0, 3), 2),
-    ("S", ("G", 7), -1),
-    ("V", ("s", 0, 512, 1), -1),
-    ("P", ("Y", 1, 0, 2), 1),
-    ("S", ("th", 0, 0, 3), -1),
-    ("V", ("s", 1, 0, 3), -1),
-    ("P", ("IU", 0, 1), 3),
-    ("S", ("th", 0, 512, 1), -1),
-    ("V", ("Q", 5), -1),
-    ("P", ("U", 6), 6),
-    ("V", ("w", 0, 0, 3), -1),
-    ("S", ("th", 1, 0, 3), -1),
-    ("V", ("w", 0, 512, 3), -1),
-    ("P", ("U", 5), 4),
-    ("V", ("w", 0, 512, 1), -1),
-    ("S", ("G", 6), -1),
-    ("V", ("Q", 4), -1),
-    ("P", ("Y", 1, 0, 1), 0),
-    ("V", ("w", 1, 0, 3), -1),
-    ("S", ("G", 5), -1),
-    ("V", ("s", 1, 0, 2), -1),
-    ("P", ("Y", 1, 640), 5),
-    ("S", ("IUc", 0, 0), -1),
-    ("V", ("s", 1, 0, 1), -1),
-    ("P", ("Y", 1, 0, 0), 2),
-    ("S", ("th", 1, 0, 2), -1),
-    ("V", ("s", 1, 640), -1),
-    ("P", ("Y", 1, 896), 6),
-    ("S", ("th", 1, 0, 1), -1),
-    ("V", ("w", 0, 0, 0), -1),
-    ("V", ("w", 1, 0, 2), -1),
-    ("P", ("U", 4), 4),
-    ("S", ("th", 1, 640), -1),
-    ("V", ("s", 1, 896), -1),
-    ("P", ("I", 0, 0, 1), 1),
-    ("S", ("IUc", 0, 1), -1),
-    ("V", ("w", 1, 0, 1), -1),
-    ("P", ("Y", 1, 512), 7),
-    ("V", ("w", 0, 512, 0), -1),
-    ("S", ("G", 4), -1),
-    ("V", ("s", 1, 0, 0), -1),
-    ("P", ("Y", 1, 768), 0),
-    ("S", ("Ic", 0, 0, 1), -1),
-    ("V", ("QU", 0), -1),
-    ("P", ("IU", 1, 1), 5),
-    ("S", ("th", 1, 0, 0), -1),
-    ("V", ("s", 1, 512), -1),
-    ("P", ("IU", 1, 0), 6),
-    ("S", ("th", 1, 896), -1),
-    ("V", ("s", 1, 768), -1),
-    ("P", ("I", 0, 0, 0), 3),
-    ("S", ("IUc", 1, 1), -1),
-    ("V", ("w", 1, 0, 0), -1),
-    ("V", ("w", 1, 896), -1),
-    ("S", ("IUc", 1, 0), -1),
-    ("P", ("I", 1, 0, 1), 4),
-    ("V", ("w", 0, 512, 2), -1),
-    ("S", ("Ic", 0, 0, 0), -1),
-    ("P", ("I", 1, 0, 0), 2),
-    ("V", ("QE", 1, 896), -1),
-    ("V", ("QU", 1), -1),
-    ("S", ("Ic", 1, 0, 1), -1),
-    ("P", ("I", 0, 512, 1), 1),
-    ("V", ("QE", 0, 0), -1),
-    ("S", ("Ic", 1, 0, 0), -1),
-    ("P", ("I", 0, 512, 0), 7),
-    ("V", ("w", 1, 640), -1),
-    ("S", ("Ic", 0, 512, 1), -1),
-    ("P", ("O", 0, 2, 0), 0),
-    ("P", ("O", 0, 0, 0), 5),
-    ("V", ("QE", 1, 0), -1),
-    ("S", ("Ic", 0, 512, 0), -1),
-    ("P", ("O", 0, 3, 0), 6),
-    ("P", ("O", 0, 1, 0), 3),
-    ("V", ("QE", 1, 640), -1),
-    ("S", ("th", 1, 512), -1),
-    ("P", ("O", 0, 1, 1), -1),
-    ("V", ("QE", 0, 512), -1),
-    ("P", ("O", 0, 2, 1), -1),
-    ("S", ("th", 1, 768), -1),
-    ("P", ("O", 0, 3, 1), -1),
-    ("V", ("w", 1, 512), -1),
-    ("P", ("O", 0, 0, 1), -1),
-    ("S", ("Oc", 0, 2), -1),
-    ("P", ("O", 512, 0, 0), 4),
-    ("P", ("O", 512, 3, 0), 2),
-    ("V", ("w", 1, 768), -1),
-    ("P", ("O", 896, 0, 0), 1),
-    ("P", ("O", 768, 0, 0), 7),
-    ("S", ("Oc", 0, 0), -1),
-    ("P", ("O", 896, 0, 1), -1),
-    ("P", ("O", 512, 2, 0), 0),
-    ("V", ("QE", 1, 512), -1),
-    ("V", ("Oc", 0, 3), -1),
-    ("S", ("Oc", 896, 0), -1),
-    ("P", ("O", 512, 2, 1), -1),
-    ("P", ("O", 512, 0, 1), -1),
-    ("P", ("O", 768, 2, 0), 5),
-    ("V", ("QE", 1, 768), -1),
-    ("P", ("O", 512, 3, 1), -1),
-    ("S", ("Oc", 512, 2), -1),
-    ("P", ("O", 896, 3, 0), 1),
-    ("V", ("Oc", 0, 1), -1),
-    ("P", ("O", 896, 2, 0), 6),
-    ("S", ("Oc", 512, 0), -1),
-    ("P", ("O", 768, 2, 1), -1),
-    ("P", ("O", 768, 0, 1), -1),
-    ("P", ("O", 896, 3, 1), -1),
-    ("P", ("O", 512, 1, 0), 0),
-    ("S", ("Oc", 768, 2), -1),
-    ("V", ("Oc", 512, 3), -1),
-    ("P", ("O", 512, 1, 1), -1),
-    ("S", ("Oc", 768, 0), -1),
-    ("P", ("O", 768, 1, 0), 4),
-    ("P", ("O", 768, 1, 1), -1),
-    ("V", ("Oc", 896, 3), -1),
-    ("P", ("O", 896, 1, 0), 3),
-    ("P", ("O", 896, 1, 1), -1),
-    ("V", ("Oc", 512, 1), -1),
-    ("P", ("O", 896, 2, 1), -1),
-    ("P", ("O", 768, 3, 0), 5),
-    ("P", ("O", 768, 3, 1), -1),
-    ("V", ("Oc", 896, 1), -1),
-    ("S", ("Oc", 896, 2), -1),
-    ("V", ("Oc", 768, 1), -1),
-    ("V", ("Oc", 768, 3), -1),
+    ("V", ("X", 0)),
+    ("S", ("X", 1)),
+    ("P", ("T", 0)),
+    ("S", ("X", 2)),
+    ("V", ("M", 0)),
+    ("P", ("T", 1)),
+    ("S", ("X", 3)),
+    ("V", ("M", 1)),
+    ("P", ("T", 2)),
+    ("S", ("X", 5)),
+    ("V", ("M", 2)),
+    ("P", ("T", 3)),
+    ("S", ("X", 4)),
+    ("V", ("Q", 0)),
+    ("V", ("M", 3)),
+    ("P", ("U", 0)),
+    ("P", ("T", 4)),
+    ("S", ("G", 0)),
+    ("V", ("Q", 1)),
+    ("P", ("T", 5)),
+    ("V", ("Q", 2)),
+    ("S", ("X", 6)),
+    ("V", ("Q", 3)),
+    ("P", ("U", 1)),
+    ("V", ("M", 5)),
+    ("P", ("Y", 0, 0)),
+    ("S", ("G", 1)),
+    ("P", ("U", 2)),
+    ("V", ("M", 4)),
+    ("P", ("Y", 0, 1)),
+    ("S", ("G", 2)),
+    ("P", ("Y", 0, 2)),
+    ("V", ("Q", 5)),
+    ("S", ("X", 7)),
+    ("V", ("s", 0, 1)),
+    ("P", ("Y", 0, 3)),
+    ("V", ("Q", 4)),
+    ("P", ("U", 3)),
+    ("S", ("th", 0, 1)),
+    ("V", ("s", 0, 2)),
+    ("P", ("T", 6)),
+    ("V", ("s", 0, 0)),
+    ("S", ("th", 0, 2)),
+    ("G", ("w", 0, 1)),
+    ("V", ("s", 0, 3)),
+    ("P", ("Y", 0, 4)),
+    ("S", ("th", 0, 0)),
+    ("V", ("M", 6)),
+    ("S", ("G", 3)),
+    ("P", ("U", 4)),
+    ("G", ("w", 0, 2)),
+    ("P", ("T", 7)),
+    ("S", ("IU", 0, 1)),
+    ("V", ("s", 0, 4)),
+    ("G", ("w", 0, 0)),
+    ("P", ("Y", 0, 5)),
+    ("V", ("M", 7)),
+    ("P", ("U", 5)),
+    ("S", ("th", 0, 3)),
+    ("P", ("Y", 0, 6)),
+    ("V", ("Q", 6)),
+    ("S", ("IU", 0, 0)),
+    ("V", ("Q", 7)),
+    ("P", ("Y", 0, 7)),
+    ("V", ("s", 0, 6)),
+    ("G", ("w", 0, 3)),
+    ("P", ("Y", 1, 0)),
+    ("V", ("s", 0, 5)),
+    ("S", ("G", 5)),
+    ("V", ("s", 0, 7)),
+    ("S", ("th", 0, 4)),
+    ("P", ("Y", 1, 1)),
+    ("V", ("QU", 0)),
+    ("S", ("th", 0, 7)),
+    ("P", ("Y", 1, 2)),
+    ("V", ("s", 1, 1)),
+    ("G", ("w", 0, 4)),
+    ("S", ("G", 4)),
+    ("P", ("Y", 1, 3)),
+    ("V", ("s", 1, 0)),
+    ("S", ("th", 1, 1)),
+    ("P", ("U", 6)),
+    ("G", ("w", 0, 7)),
+    ("V", ("s", 1, 3)),
+    ("S", ("th", 1, 0)),
+    ("P", ("Y", 1, 4)),
+    ("V", ("s", 1, 2)),
+    ("S", ("th", 1, 3)),
+    ("P", ("Y", 1, 5)),
+    ("V", ("w", 1, 0)),
+    ("S", ("th", 0, 5)),
+    ("P", ("U", 7)),
+    ("V", ("w", 1, 3)),
+    ("S", ("G", 6)),
+    ("P", ("Y", 1, 6)),
+    ("V", ("w", 1, 1)),
+    ("S", ("th", 0, 6)),
+    ("P", ("Y", 1, 7)),
+    ("V", ("QE", 0, 0)),
+    ("S", ("G", 7)),
+    ("V", ("s", 1, 4)),
+    ("G", ("w", 0, 5)),
+    ("P", ("O", 0, 0, 0)),
+    ("S", ("th", 1, 2)),
+    ("V", ("s", 1, 5)),
+    ("S", ("IU", 1, 0)),
+    ("G", ("w", 0, 6)),
+    ("V", ("s", 1, 7)),
+    ("V", ("s", 1, 6)),
+    ("S", ("IU", 1, 1)),
+    ("V", ("w", 1, 2)),
+    ("V", ("QE", 0, 4)),
+    ("S", ("th", 1, 7)),
+    ("V", ("QE", 1, 0)),
+    ("S", ("th", 1, 4)),
+    ("V", ("QU", 1)),
+    ("S", ("th", 1, 5)),
+    ("V", ("w", 1, 4)),
+    ("P", ("O", 0, 0, 1)),
+    ("S", ("th", 1, 6)),
+    ("P", ("O", 0, 1, 0)),
+    ("V", ("w", 1, 5)),
+    ("P", ("O", 0, 1, 1)),
+    ("S", ("Oc", 0, 0)),
+    ("P", ("O", 0, 2, 0)),
+    ("V", ("w", 1, 6)),
+    ("P", ("O", 0, 2, 1)),
+    ("P", ("O", 0, 3, 0)),
+    ("S", ("Oc", 0, 2)),
+    ("V", ("QE", 1, 4)),
+    ("P", ("O", 0, 3, 1)),
+    ("P", ("O", 4, 0, 0)),
+    ("V", ("w", 1, 7)),
+    ("S", ("Oc", 0, 1)),
+    ("P", ("O", 4, 0, 1)),
+    ("P", ("O", 4, 1, 0)),
+    ("P", ("O", 4, 1, 1)),
+    ("P", ("O", 4, 2, 0)),
+    ("P", ("O", 4, 2, 1)),
+    ("S", ("Oc", 0, 3)),
+    ("V", ("QE", 1, 6)),
+    ("P", ("O", 4, 3, 0)),
+    ("P", ("O", 4, 3, 1)),
+    ("P", ("O", 6, 0, 0)),
+    ("V", ("Oc", 4, 1)),
+    ("S", ("Oc", 4, 0)),
+    ("P", ("O", 6, 0, 1)),
+    ("V", ("Oc", 4, 3)),
+    ("P", ("O", 6, 1, 0)),
+    ("P", ("O", 6, 1, 1)),
+    ("S", ("Oc", 4, 2)),
+    ("P", ("O", 6, 2, 0)),
+    ("V", ("Oc", 6, 0)),
+    ("P", ("O", 6, 2, 1)),
+    ("S", ("Oc", 6, 1)),
+    ("P", ("O", 6, 3, 0)),
+    ("P", ("O", 6, 3, 1)),
+    ("V", ("Oc", 6, 2)),
+    ("S", ("Oc", 6, 3)),
 ]
 
 
@@ -225,11 +191,14 @@ def tile_lorafalogcoshgradient_w4_kernel(
     nc = tc.nc
     with ExitStack() as ctx:
         keep = ctx.enter_context(tc.tile_pool(name="keep", bufs=1))
-        wide = ctx.enter_context(tc.tile_pool(name="wide", bufs=8))
-        zs = ctx.enter_context(tc.tile_pool(name="zs", bufs=10))
-        grp = ctx.enter_context(tc.tile_pool(name="grp", bufs=3))
-        outs = ctx.enter_context(tc.tile_pool(name="outs", bufs=6))
-        ps = ctx.enter_context(tc.psum_pool(name="ps", bufs=1))
+        xpool = ctx.enter_context(tc.tile_pool(name="xpool", bufs=8))
+        zs = ctx.enter_context(tc.tile_pool(name="zs", bufs=8))
+        outs = ctx.enter_context(tc.tile_pool(name="outs", bufs=8))
+        psums = {
+            "T": ctx.enter_context(tc.psum_pool(name="pt", bufs=2)),
+            "Y": ctx.enter_context(tc.psum_pool(name="py", bufs=4)),
+            "B": ctx.enter_context(tc.psum_pool(name="pb", bufs=2)),
+        }
         ctx.enter_context(tc.manual_schedule())
 
         warm = keep.tile([P, 1], F32)
@@ -239,16 +208,14 @@ def tile_lorafalogcoshgradient_w4_kernel(
         a_sc = keep.tile([P, 2, R], U8, align_bytes=64)
         nc.vector.memset(wm_sc[:].rearrange("p c n -> p (c n)").bitcast(I32), 0)
         nc.vector.memset(a_sc[:].rearrange("p c n -> p (c n)").bitcast(I32), 0)
-        ident_f = keep.tile([P, P], F32)
-        make_identity(nc, ident_f[:])
-        ident_b = keep.tile([P, P], BF16)
-        make_identity(nc, ident_b[:])
+        ident = keep.tile([P, P], F32)
+        make_identity(nc, ident[:])
 
         xb_view = x_bytes.rearrange("(g p t) k -> g p t k", p=P, t=4)
         tg_view = target.rearrange("(g p t) f -> g p t f", p=P, t=4)
         xb = [keep.tile([P, D], U8, align_bytes=64, name=f"xb{i}") for i in range(8)]
         tg = [keep.tile([P, 4, F], BF16, name=f"tg{i}") for i in range(2)]
-        xs = keep.tile([P, D], F32)
+        xsp = keep.tile([P, 2, 4], F32)
         wm_w = keep.tile([P, 2, 2 * F], U8, align_bytes=64)
         a_w = keep.tile([P, 2, 2 * R], U8, align_bytes=64)
         s_b = keep.tile([P, 2, 4], BF16)
@@ -269,30 +236,25 @@ def tile_lorafalogcoshgradient_w4_kernel(
                     in_=src[:, 4 * q : 4 * q + 4, :].rearrange("g q n -> q g n").bitcast(I32),
                 )
 
-        def load_xs(c):
-            nc.sync.dma_start(
-                out=xs[:, 512 * c : 512 * (c + 1)],
-                in_=x_scale[:, 512 * c : 512 * (c + 1)].rearrange("o k -> (o k)").partition_broadcast(P),
-            )
-
         load_x(0)
-        load_xs(0)
-        load_xs(1)
         load_x(1)
+        nc.sync.dma_start(out=xsp[:], in_=x_scale.rearrange("o (c p t) -> p (o c) t", p=P, t=4))
+        load_x(2)
+        load_x(3)
+        load_x(4)
         load_scales(wm_sc, wm_scales)
         nc.sync.dma_start(out=wm_w[:, 0, :], in_=wm_words[0])
         nc.sync.dma_start(out=wm_w[:, 1, :], in_=wm_words[1])
-        load_x(2)
-        load_x(3)
+        load_x(5)
         load_scales(a_sc, a_scales)
-        nc.sync.dma_start(out=s_b[:], in_=s.rearrange("(g p t) -> p g t", p=P, t=4))
         nc.sync.dma_start(out=a_w[:, 0, :], in_=a_words[0])
         nc.sync.dma_start(out=a_w[:, 1, :], in_=a_words[1])
+        nc.sync.dma_start(out=s_b[:], in_=s.rearrange("(g p t) -> p g t", p=P, t=4))
+        load_x(6)
+        load_x(7)
         for i in range(4):
             load_t(i)
         nc.sync.dma_start(out=wt_b[:], in_=wt.rearrange("(g p t) -> p g t", p=P, t=4))
-        for i in range(4, 8):
-            load_x(i)
         for i in range(4, 8):
             load_t(i)
         nc.gpsimd.tensor_copy(out=s_f[:], in_=s_b[:])
@@ -300,8 +262,11 @@ def tile_lorafalogcoshgradient_w4_kernel(
 
         x_codes = [keep.tile([P, 2 * P], U32, align_bytes=64, name=f"xc{i}") for i in range(8)]
         x_sc = [keep.tile([P, 2 * P], U8, align_bytes=64, name=f"xsc{i}") for i in range(8)]
+        e_bf = [keep.tile([P, 4 * F], BF16, align_bytes=64, name=f"eb{i}") for i in range(2)]
         e_codes = [keep.tile([P, F], U32, align_bytes=64, name=f"ec{i}") for i in range(2)]
         e_sc = [keep.tile([P, F], U8, align_bytes=64, name=f"esc{i}") for i in range(2)]
+        ugp = [keep.tile([P, 4, R], BF16, name=f"up{i}") for i in range(2)]
+        ug_bf = [keep.tile([P, 4 * R], BF16, align_bytes=64, name=f"ub{i}") for i in range(2)]
         u_codes = [keep.tile([P, R], U32, align_bytes=64, name=f"uc{i}") for i in range(2)]
         u_sc = [keep.tile([P, R], U8, align_bytes=64, name=f"usc{i}") for i in range(2)]
         val = {}
@@ -318,170 +283,126 @@ def tile_lorafalogcoshgradient_w4_kernel(
                     stop=(c == 1),
                 )
 
-        def interleave(dst, planar, h):
-            for j in range(2):
-                lo = 256 * h + 128 * j
-                nc.tensor.matmul(
-                    out=dst[:, 512 * j : 512 * (j + 1)].rearrange("p (f t) -> p f t", t=4),
-                    lhsT=ident_b[:],
-                    rhs=planar[:, :, lo : lo + 128].rearrange("p t f -> p f t"),
-                    start=True,
-                    stop=True,
-                )
-
-        def run(eng, tok, b):
+        def run(eng, tok):
             kind = tok[0]
-            if b >= 0:
-                if kind == "T":
-                    bank = ps.tile([P, 2, 2, P], F32, name=f"bank{b}")
-                    val["T", tok[1]] = bank
-                elif kind == "Y" and len(tok) == 3:
-                    bank = ps.tile([P, 4, P], F32, name=f"bank{b}")
-                elif kind in ("I", "IU"):
-                    bank = ps.tile([P, 1024], BF16, name=f"bank{b}")
+            if kind == "X":
+                i = tok[1]
+                xw = xpool.tile([P, D], BF16, align_bytes=64, name="xw")
+                val["X", i] = xw
+                if eng == "V":
+                    nc.vector.tensor_copy(out=xw[:], in_=xb[i][:].bitcast(F8))
                 else:
-                    bank = ps.tile([P, 512], F32, name=f"bank{b}")
-            if kind == "W":
-                i, c = tok[1], tok[2]
-                lo, hi = (512 * c, 512 * c + 512) if i in WSPLIT else (0, 1024)
-                if ("W", i) not in val:
-                    xw = wide.tile([P, D], BF16, align_bytes=64, name="xw")
-                    val["W", i] = xw
-                nc.vector.tensor_tensor(out=val["W", i][:, lo:hi], in0=xb[i][:, lo:hi].bitcast(F8), in1=xs[:, lo:hi], op=MULT)
+                    nc.scalar.copy(out=xw[:], in_=xb[i][:].bitcast(F8))
             elif kind == "T":
                 i = tok[1]
-                words = val["W", i][:].bitcast(F32)
-                for c in (tok[2],) if i in WSPLIT else (0, 1):
+                words = val["X", i][:].bitcast(F32)
+                bank = psums["T"].tile([P, 2, 2 * P], F32, name="t_bank")
+                val[tok] = bank
+                for c in range(2):
                     for u in range(2):
-                        nc.tensor.transpose(val["T", i][:, c, u, :], words[:, 256 * c + u : 256 * (c + 1) : 2], ident_f[:])
-            elif kind == "C":
+                        nc.tensor.transpose(
+                            bank[:, u, P * c : P * (c + 1)], words[:, 256 * c + u : 256 * (c + 1) : 2], ident[:]
+                        )
+            elif kind == "M":
                 i = tok[1]
-                xt = wide.tile([P, D], BF16, align_bytes=64, name="xt")
-                val["C", i] = xt
-                nc.scalar.copy(
-                    out=xt[:].bitcast(F32).rearrange("p (c r u) -> p c r u", c=2, u=2),
-                    in_=val["T", i][:].rearrange("p c u r -> p c r u"),
+                xt = xpool.tile([P, D], BF16, align_bytes=64, name="xt")
+                val[tok] = xt
+                nc.vector.tensor_tensor(
+                    out=xt[:].rearrange("p (c r u e) -> p c r u e", c=2, u=2, e=2),
+                    in0=val["T", i][:].bitcast(BF16).rearrange("p u (c r e) -> p c r u e", c=2, e=2),
+                    in1=xsp[:].rearrange("p c (u e) -> p c u e", u=2).unsqueeze(2).to_broadcast([P, 2, P, 2, 2]),
+                    op=MULT,
                 )
             elif kind == "Q":
                 i = tok[1]
-                nc.vector.quantize_mx(out=x_codes[i][:].bitcast(F8X4), scales=x_sc[i][:], in_=val["C", i][:])
+                nc.vector.quantize_mx(out=x_codes[i][:].bitcast(F8X4), scales=x_sc[i][:], in_=val["M", i][:])
             elif kind == "U":
+                bank = psums["B"].tile([P, 512], F32, name="b_bank")
                 val[tok] = bank
-                mm(bank[:], tok[1], a_w, a_sc, 0, 512)
+                mm(bank[:], tok[1], a_w, a_sc, 0, R)
             elif kind == "G":
                 i = tok[1]
                 g, t = divmod(i, 4)
-                if ("up", g) not in val:
-                    up = grp.tile([P, 4, 512], BF16, name="up")
-                    val["up", g] = up
-                nc.scalar.activation(out=val["up", g][:, t, :], in_=val["U", i][:], func=ACT.Copy, scale=s_f[:, g, t : t + 1])
+                nc.scalar.activation(out=ugp[g][:, t, :], in_=val["U", i][:], func=ACT.Copy, scale=s_f[:, g, t : t + 1])
             elif kind == "IU":
-                val[tok] = bank
-                interleave(bank, val["up", tok[1]], tok[2])
-            elif kind == "IUc":
-                g, h = tok[1], tok[2]
-                if ("ui", g) not in val:
-                    ui = grp.tile([P, 2048], BF16, align_bytes=64, name="ui")
-                    val["ui", g] = ui
-                nc.scalar.copy(out=val["ui", g][:, 1024 * h : 1024 * (h + 1)], in_=val["IU", g, h][:])
+                g, h = tok[1:]
+                nc.scalar.copy(
+                    out=ug_bf[g][:, 1024 * h : 1024 * (h + 1)].rearrange("p (c i t) -> p c t i", i=4, t=4),
+                    in_=ugp[g][:, :, 256 * h : 256 * (h + 1)].rearrange("p t (c i) -> p c t i", i=4),
+                )
             elif kind == "QU":
                 g = tok[1]
-                nc.vector.quantize_mx(out=u_codes[g][:].bitcast(F8X4), scales=u_sc[g][:], in_=val["ui", g][:])
+                nc.vector.quantize_mx(out=u_codes[g][:].bitcast(F8X4), scales=u_sc[g][:], in_=ug_bf[g][:])
             elif kind == "Y":
+                g, j = tok[1:]
+                bank = psums["Y"].tile([P, 4, P], F32, name="y_bank")
                 val[tok] = bank
-                g, f0 = tok[1], tok[2]
-                if len(tok) == 4:
-                    mm(bank[:], 4 * g + tok[3], wm_w, wm_sc, f0, f0 + 512)
-                else:
-                    for t in range(4):
-                        mm(bank[:, t, :], 4 * g + t, wm_w, wm_sc, f0, f0 + P)
+                for t in range(4):
+                    mm(bank[:, t, :], 4 * g + t, wm_w, wm_sc, P * j, P * (j + 1))
             elif kind == "s":
-                g, f0 = tok[1], tok[2]
+                g, j = tok[1:]
                 z = zs.tile([P, 512], F32, name="z")
                 val[tok] = z
-                if len(tok) == 4:
-                    nc.vector.tensor_tensor(out=z[:], in0=val[("Y",) + tok[1:]][:], in1=tg[g][:, tok[3], f0 : f0 + 512], op=SUB)
-                else:
-                    nc.vector.tensor_tensor(
-                        out=z[:].rearrange("p (f t) -> p f t", t=4),
-                        in0=val[("Y",) + tok[1:]][:].rearrange("p t f -> p f t"),
-                        in1=tg[g][:, :, f0 : f0 + P].rearrange("p t f -> p f t"),
-                        op=SUB,
-                    )
+                nc.vector.tensor_tensor(
+                    out=z[:].rearrange("p (f t) -> p f t", t=4),
+                    in0=val["Y", g, j][:].rearrange("p t f -> p f t"),
+                    in1=tg[g][:, :, P * j : P * (j + 1)].rearrange("p t f -> p f t"),
+                    op=SUB,
+                )
             elif kind == "th":
+                g, j = tok[1:]
                 th = zs.tile([P, 512], F32, name="th")
                 val[tok] = th
-                nc.scalar.activation(out=th[:], in_=val[("s",) + tok[1:]][:], func=ACT.Tanh)
+                nc.scalar.activation(out=th[:], in_=val["s", g, j][:], func=ACT.Tanh)
             elif kind == "w":
-                g, f0 = tok[1], tok[2]
-                if len(tok) == 4:
-                    t = tok[3]
-                    if ("ep", g, f0) not in val:
-                        ep = grp.tile([P, 4, 512], BF16, name="ep")
-                        val["ep", g, f0] = ep
-                    dst = val["ep", g, f0][:, t, :]
-                    src = val[("th",) + tok[1:]][:]
-                    if eng == "V":
-                        nc.vector.tensor_scalar(out=dst, in0=src, scalar1=wt_f[:, g, t : t + 1], scalar2=None, op0=MULT)
-                    elif eng == "G":
-                        nc.gpsimd.tensor_scalar(out=dst, in0=src, scalar1=wt_f[:, g, t : t + 1], scalar2=0.0, op0=MULT, op1=ADD)
-                    else:
-                        nc.scalar.activation(out=dst, in_=src, func=ACT.Copy, scale=wt_f[:, g, t : t + 1])
-                else:
-                    ei = zs.tile([P, 512], BF16, align_bytes=64, name="ei")
-                    val[tok] = ei
-                    nc.vector.tensor_tensor(
-                        out=ei[:].rearrange("p (f t) -> p f t", t=4),
-                        in0=val[("th",) + tok[1:]][:].rearrange("p (f t) -> p f t", t=4),
-                        in1=wt_f[:, g, :].unsqueeze(1).to_broadcast([P, P, 4]),
-                        op=MULT,
-                    )
-            elif kind == "I":
-                val[tok] = bank
-                interleave(bank, val["ep", tok[1], tok[2]], tok[3])
-            elif kind == "Ic":
-                g, f0, h = tok[1:]
-                if ("ei", g, f0) not in val:
-                    eint = grp.tile([P, 2048], BF16, align_bytes=64, name="eint")
-                    val["ei", g, f0] = eint
-                dst = val["ei", g, f0][:, 1024 * h : 1024 * (h + 1)]
-                if eng == "V":
-                    nc.vector.tensor_copy(out=dst, in_=val["I", g, f0, h][:])
-                else:
-                    nc.scalar.copy(out=dst, in_=val["I", g, f0, h][:])
+                g, j = tok[1:]
+                engine = nc.vector if eng == "V" else nc.gpsimd
+                engine.tensor_tensor(
+                    out=e_bf[g][:, 512 * j : 512 * (j + 1)].rearrange("p (f t) -> p f t", t=4),
+                    in0=val["th", g, j][:].rearrange("p (f t) -> p f t", t=4),
+                    in1=wt_f[:, g, :].unsqueeze(1).to_broadcast([P, P, 4]),
+                    op=MULT,
+                )
             elif kind == "QE":
-                g, f0 = tok[1], tok[2]
-                if ("ei", g, f0) in val:
-                    src, n = val["ei", g, f0], 512
-                else:
-                    src, n = val[("w",) + tok[1:]], P
+                g, j = tok[1:]
+                n = QE_SPAN[g, j]
                 nc.vector.quantize_mx(
-                    out=e_codes[g][:, f0 : f0 + n].bitcast(F8X4), scales=e_sc[g][:, f0 : f0 + n], in_=src[:]
+                    out=e_codes[g][:, P * j : P * (j + n)].bitcast(F8X4),
+                    scales=e_sc[g][:, P * j : P * (j + n)],
+                    in_=e_bf[g][:, 512 * j : 512 * (j + n)],
                 )
             elif kind == "O":
-                f0, rt, g = tok[1:]
-                n = O_WIDTH[f0]
+                j, rt, g = tok[1:]
+                n = P * O_SPAN[j]
                 if g == 0:
-                    val["O", f0, rt] = bank
+                    tag = O_POOL[j][rt]
+                    if tag == "T":
+                        bank = psums["T"].tile([P, 512], F32, name="t_bank")
+                    elif tag == "B":
+                        bank = psums["B"].tile([P, 512], F32, name="b_bank")
+                    else:
+                        bank = psums["Y"].tile([P, 512], F32, name="y_bank")
+                    val["O", j, rt] = bank
                 nc.tensor.matmul_mx(
-                    out=val["O", f0, rt][:, 0:n],
+                    out=val["O", j, rt][:, 0:n],
                     lhsT=u_codes[g][:, P * rt : P * (rt + 1)].bitcast(F8X4),
                     lhsT_scale=u_sc[g][:, P * rt : P * (rt + 1)],
-                    rhs=e_codes[g][:, f0 : f0 + n].bitcast(F8X4),
-                    rhs_scale=e_sc[g][:, f0 : f0 + n],
+                    rhs=e_codes[g][:, P * j : P * j + n].bitcast(F8X4),
+                    rhs_scale=e_sc[g][:, P * j : P * j + n],
                     start=(g == 0),
                     stop=(g == 1),
                 )
             elif kind == "Oc":
-                f0, rt = tok[1:]
-                n = O_WIDTH[f0]
+                j, rt = tok[1:]
+                n = P * O_SPAN[j]
                 res = outs.tile([P, 512], F32, name="res")
-                src = val["O", f0, rt][:, 0:n]
                 if eng == "S":
-                    nc.scalar.activation(out=res[:, 0:n], in_=src, func=ACT.Copy, scale=1.0 / 32.0)
+                    nc.scalar.activation(out=res[:, 0:n], in_=val["O", j, rt][:, 0:n], func=ACT.Copy, scale=1.0 / 32.0)
                 else:
-                    nc.vector.tensor_scalar(out=res[:, 0:n], in0=src, scalar1=1.0 / 32.0, scalar2=None, op0=MULT)
-                nc.sync.dma_start(out=out[P * rt : P * (rt + 1), f0 : f0 + n], in_=res[:, 0:n])
+                    nc.vector.tensor_scalar(
+                        out=res[:, 0:n], in0=val["O", j, rt][:, 0:n], scalar1=1.0 / 32.0, scalar2=None, op0=MULT
+                    )
+                nc.sync.dma_start(out=out[P * rt : P * (rt + 1), P * j : P * j + n], in_=res[:, 0:n])
 
-        for eng, tok, b in ORDER:
-            run(eng, tok, b)
+        for eng, tok in ORDER:
+            run(eng, tok)

@@ -23,163 +23,165 @@ O_SPAN = {0: 4, 4: 2, 6: 2}
 O_POOL = {0: "TTBB", 4: "YYYY", 6: "TTBB"}
 
 ORDER = [
-    ("V", ("X", 0)),
+    ("V", ("Xa", 0)),
+    ("S", ("Xb", 0)),
+    ("P", ("Ta", 0)),
     ("S", ("X", 1)),
     ("P", ("T", 0)),
-    ("S", ("X", 2)),
     ("V", ("M", 0)),
+    ("S", ("X", 2)),
     ("P", ("T", 1)),
+    ("V", ("Q", 0)),
     ("S", ("X", 3)),
     ("V", ("M", 1)),
     ("P", ("T", 2)),
     ("S", ("X", 5)),
     ("V", ("M", 2)),
     ("P", ("T", 3)),
-    ("S", ("X", 4)),
-    ("V", ("Q", 0)),
-    ("V", ("M", 3)),
     ("P", ("U", 0)),
-    ("P", ("T", 4)),
-    ("S", ("G", 0)),
+    ("S", ("X", 4)),
     ("V", ("Q", 1)),
-    ("P", ("T", 5)),
-    ("V", ("Q", 2)),
-    ("S", ("X", 6)),
-    ("V", ("Q", 3)),
+    ("V", ("M", 3)),
     ("P", ("U", 1)),
-    ("V", ("M", 5)),
-    ("P", ("Y", 0, 0)),
-    ("S", ("G", 1)),
-    ("P", ("U", 2)),
-    ("V", ("M", 4)),
-    ("P", ("Y", 0, 1)),
-    ("S", ("G", 2)),
-    ("P", ("Y", 0, 2)),
-    ("V", ("Q", 5)),
     ("S", ("X", 7)),
-    ("V", ("s", 0, 1)),
-    ("P", ("Y", 0, 3)),
-    ("V", ("Q", 4)),
-    ("P", ("U", 3)),
-    ("S", ("th", 0, 1)),
-    ("V", ("s", 0, 2)),
-    ("P", ("T", 6)),
+    ("P", ("T", 4)),
+    ("V", ("Q", 2)),
+    ("P", ("T", 5)),
+    ("V", ("Q", 3)),
+    ("S", ("G", 1)),
+    ("V", ("M", 4)),
+    ("P", ("Y", 0, 0)),
+    ("S", ("X", 6)),
+    ("P", ("Y", 0, 1)),
     ("V", ("s", 0, 0)),
+    ("P", ("Y", 0, 2)),
+    ("V", ("Q", 4)),
+    ("S", ("th", 0, 0)),
+    ("P", ("Y", 0, 3)),
+    ("V", ("s", 0, 1)),
+    ("S", ("G", 0)),
+    ("P", ("Y", 0, 4)),
+    ("V", ("s", 0, 2)),
+    ("G", ("w", 0, 0)),
+    ("S", ("th", 0, 1)),
+    ("V", ("M", 5)),
+    ("P", ("U", 2)),
     ("S", ("th", 0, 2)),
+    ("P", ("Y", 0, 5)),
     ("G", ("w", 0, 1)),
     ("V", ("s", 0, 3)),
-    ("P", ("Y", 0, 4)),
-    ("S", ("th", 0, 0)),
-    ("V", ("M", 6)),
-    ("S", ("G", 3)),
-    ("P", ("U", 4)),
-    ("G", ("w", 0, 2)),
-    ("P", ("T", 7)),
-    ("S", ("IU", 0, 1)),
-    ("V", ("s", 0, 4)),
-    ("G", ("w", 0, 0)),
-    ("P", ("Y", 0, 5)),
-    ("V", ("M", 7)),
-    ("P", ("U", 5)),
-    ("S", ("th", 0, 3)),
-    ("P", ("Y", 0, 6)),
-    ("V", ("Q", 6)),
-    ("S", ("IU", 0, 0)),
-    ("V", ("Q", 7)),
-    ("P", ("Y", 0, 7)),
-    ("V", ("s", 0, 6)),
-    ("G", ("w", 0, 3)),
-    ("P", ("Y", 1, 0)),
+    ("S", ("G", 2)),
+    ("P", ("U", 3)),
     ("V", ("s", 0, 5)),
-    ("S", ("G", 5)),
-    ("V", ("s", 0, 7)),
+    ("P", ("T", 6)),
+    ("G", ("w", 0, 2)),
+    ("S", ("G", 3)),
+    ("V", ("s", 0, 4)),
+    ("P", ("Y", 0, 6)),
+    ("S", ("th", 0, 3)),
+    ("V", ("M", 6)),
+    ("P", ("T", 7)),
+    ("S", ("IU", 0, 0)),
+    ("G", ("w", 0, 3)),
+    ("P", ("U", 4)),
+    ("V", ("s", 0, 6)),
+    ("P", ("Y", 0, 7)),
+    ("V", ("M", 7)),
     ("S", ("th", 0, 4)),
-    ("P", ("Y", 1, 1)),
-    ("V", ("QU", 0)),
-    ("S", ("th", 0, 7)),
-    ("P", ("Y", 1, 2)),
-    ("V", ("s", 1, 1)),
-    ("G", ("w", 0, 4)),
+    ("S", ("IU", 0, 1)),
+    ("V", ("Q", 6)),
+    ("V", ("Q", 5)),
+    ("V", ("Q", 7)),
+    ("S", ("th", 0, 5)),
+    ("P", ("U", 5)),
+    ("V", ("QE", 0, 0)),
+    ("P", ("Y", 1, 0)),
     ("S", ("G", 4)),
-    ("P", ("Y", 1, 3)),
+    ("V", ("QU", 0)),
+    ("P", ("Y", 1, 1)),
+    ("S", ("th", 0, 6)),
+    ("V", ("s", 0, 7)),
+    ("G", ("w", 0, 5)),
+    ("P", ("Y", 1, 2)),
+    ("S", ("G", 5)),
     ("V", ("s", 1, 0)),
-    ("S", ("th", 1, 1)),
-    ("P", ("U", 6)),
-    ("G", ("w", 0, 7)),
-    ("V", ("s", 1, 3)),
-    ("S", ("th", 1, 0)),
+    ("P", ("Y", 1, 3)),
+    ("S", ("th", 0, 7)),
+    ("G", ("w", 0, 4)),
+    ("V", ("s", 1, 1)),
     ("P", ("Y", 1, 4)),
     ("V", ("s", 1, 2)),
-    ("S", ("th", 1, 3)),
+    ("S", ("th", 1, 0)),
     ("P", ("Y", 1, 5)),
-    ("V", ("w", 1, 0)),
-    ("S", ("th", 0, 5)),
-    ("P", ("U", 7)),
-    ("V", ("w", 1, 3)),
-    ("S", ("G", 6)),
-    ("P", ("Y", 1, 6)),
-    ("V", ("w", 1, 1)),
-    ("S", ("th", 0, 6)),
-    ("P", ("Y", 1, 7)),
-    ("V", ("QE", 0, 0)),
-    ("S", ("G", 7)),
-    ("V", ("s", 1, 4)),
-    ("G", ("w", 0, 5)),
-    ("P", ("O", 0, 0, 0)),
+    ("G", ("w", 0, 7)),
+    ("V", ("s", 1, 3)),
     ("S", ("th", 1, 2)),
-    ("V", ("s", 1, 5)),
-    ("S", ("IU", 1, 0)),
+    ("P", ("U", 6)),
+    ("V", ("s", 1, 4)),
+    ("S", ("th", 1, 3)),
+    ("P", ("Y", 1, 6)),
     ("G", ("w", 0, 6)),
-    ("V", ("s", 1, 7)),
-    ("V", ("s", 1, 6)),
-    ("S", ("IU", 1, 1)),
-    ("V", ("w", 1, 2)),
-    ("V", ("QE", 0, 4)),
-    ("S", ("th", 1, 7)),
-    ("V", ("QE", 1, 0)),
+    ("V", ("s", 1, 5)),
+    ("P", ("Y", 1, 7)),
     ("S", ("th", 1, 4)),
-    ("V", ("QU", 1)),
+    ("V", ("s", 1, 6)),
+    ("P", ("U", 7)),
+    ("S", ("th", 1, 1)),
+    ("V", ("s", 1, 7)),
+    ("P", ("O", 0, 0, 0)),
+    ("S", ("G", 6)),
+    ("P", ("O", 0, 1, 0)),
+    ("V", ("w", 1, 2)),
+    ("S", ("G", 7)),
+    ("V", ("w", 1, 0)),
+    ("P", ("O", 0, 2, 0)),
     ("S", ("th", 1, 5)),
     ("V", ("w", 1, 4)),
-    ("P", ("O", 0, 0, 1)),
+    ("P", ("O", 0, 3, 0)),
+    ("V", ("w", 1, 1)),
+    ("S", ("IU", 1, 0)),
+    ("V", ("w", 1, 3)),
+    ("V", ("QE", 0, 4)),
     ("S", ("th", 1, 6)),
-    ("P", ("O", 0, 1, 0)),
     ("V", ("w", 1, 5)),
+    ("S", ("IU", 1, 1)),
+    ("V", ("w", 1, 6)),
+    ("V", ("QE", 1, 0)),
+    ("S", ("th", 1, 7)),
+    ("V", ("QU", 1)),
+    ("V", ("QE", 1, 4)),
+    ("P", ("O", 0, 0, 1)),
+    ("V", ("w", 1, 7)),
     ("P", ("O", 0, 1, 1)),
     ("S", ("Oc", 0, 0)),
-    ("P", ("O", 0, 2, 0)),
-    ("V", ("w", 1, 6)),
     ("P", ("O", 0, 2, 1)),
-    ("P", ("O", 0, 3, 0)),
-    ("S", ("Oc", 0, 2)),
-    ("V", ("QE", 1, 4)),
+    ("V", ("Oc", 0, 1)),
     ("P", ("O", 0, 3, 1)),
     ("P", ("O", 4, 0, 0)),
-    ("V", ("w", 1, 7)),
-    ("S", ("Oc", 0, 1)),
-    ("P", ("O", 4, 0, 1)),
+    ("S", ("Oc", 0, 2)),
     ("P", ("O", 4, 1, 0)),
-    ("P", ("O", 4, 1, 1)),
     ("P", ("O", 4, 2, 0)),
-    ("P", ("O", 4, 2, 1)),
-    ("S", ("Oc", 0, 3)),
-    ("V", ("QE", 1, 6)),
+    ("V", ("Oc", 0, 3)),
     ("P", ("O", 4, 3, 0)),
+    ("P", ("O", 4, 0, 1)),
+    ("P", ("O", 4, 1, 1)),
+    ("P", ("O", 4, 2, 1)),
+    ("V", ("QE", 1, 6)),
+    ("S", ("Oc", 4, 0)),
     ("P", ("O", 4, 3, 1)),
     ("P", ("O", 6, 0, 0)),
-    ("V", ("Oc", 4, 1)),
-    ("S", ("Oc", 4, 0)),
-    ("P", ("O", 6, 0, 1)),
-    ("V", ("Oc", 4, 3)),
     ("P", ("O", 6, 1, 0)),
-    ("P", ("O", 6, 1, 1)),
     ("S", ("Oc", 4, 2)),
+    ("V", ("Oc", 4, 3)),
     ("P", ("O", 6, 2, 0)),
-    ("V", ("Oc", 6, 0)),
-    ("P", ("O", 6, 2, 1)),
-    ("S", ("Oc", 6, 1)),
     ("P", ("O", 6, 3, 0)),
+    ("P", ("O", 6, 0, 1)),
+    ("V", ("Oc", 4, 1)),
+    ("P", ("O", 6, 1, 1)),
+    ("P", ("O", 6, 2, 1)),
+    ("V", ("Oc", 6, 0)),
     ("P", ("O", 6, 3, 1)),
+    ("S", ("Oc", 6, 1)),
     ("V", ("Oc", 6, 2)),
     ("S", ("Oc", 6, 3)),
 ]
@@ -213,7 +215,7 @@ def tile_lorafalogcoshgradient_w4_kernel(
 
         xb_view = x_bytes.rearrange("(g p t) k -> g p t k", p=P, t=4)
         tg_view = target.rearrange("(g p t) f -> g p t f", p=P, t=4)
-        xb = [keep.tile([P, D], U8, align_bytes=64, name=f"xb{i}") for i in range(8)]
+        xb = [keep.tile([P, n, D], U8, align_bytes=64, name=f"xb{i}") for i, n in ((0, 1), (1, 1), (2, 2), (4, 2), (6, 2))]
         tg = [keep.tile([P, 4, F], BF16, name=f"tg{i}") for i in range(2)]
         xsp = keep.tile([P, 2, 4], F32)
         wm_w = keep.tile([P, 2, 2 * F], U8, align_bytes=64)
@@ -223,11 +225,10 @@ def tile_lorafalogcoshgradient_w4_kernel(
         s_f = keep.tile([P, 2, 4], F32)
         wt_f = keep.tile([P, 2, 4], F32)
 
-        def load_x(i):
-            nc.sync.dma_start(out=xb[i][:], in_=xb_view[i // 4, :, i % 4, :])
+        xsrc = [xb[0][:, 0, :], xb[1][:, 0, :]] + [xb[1 + i // 2][:, i % 2, :] for i in range(2, 8)]
 
-        def load_t(i):
-            nc.sync.dma_start(out=tg[i // 4][:, i % 4, :], in_=tg_view[i // 4, :, i % 4, :])
+        def load_x(j, i, n):
+            nc.sync.dma_start(out=xb[j][:], in_=xb_view[i // 4, :, i % 4 : i % 4 + n, :])
 
         def load_scales(dst, src):
             for q in range(4):
@@ -236,27 +237,20 @@ def tile_lorafalogcoshgradient_w4_kernel(
                     in_=src[:, 4 * q : 4 * q + 4, :].rearrange("g q n -> q g n").bitcast(I32),
                 )
 
-        load_x(0)
-        load_x(1)
+        load_x(0, 0, 1)
+        load_x(1, 1, 1)
         nc.sync.dma_start(out=xsp[:], in_=x_scale.rearrange("o (c p t) -> p (o c) t", p=P, t=4))
-        load_x(2)
-        load_x(3)
-        load_x(4)
+        load_x(2, 2, 2)
         load_scales(wm_sc, wm_scales)
-        nc.sync.dma_start(out=wm_w[:, 0, :], in_=wm_words[0])
-        nc.sync.dma_start(out=wm_w[:, 1, :], in_=wm_words[1])
-        load_x(5)
+        nc.sync.dma_start(out=wm_w[:], in_=wm_words.rearrange("c p b -> p c b"))
+        load_x(3, 4, 2)
+        load_x(4, 6, 2)
         load_scales(a_sc, a_scales)
-        nc.sync.dma_start(out=a_w[:, 0, :], in_=a_words[0])
-        nc.sync.dma_start(out=a_w[:, 1, :], in_=a_words[1])
+        nc.sync.dma_start(out=a_w[:], in_=a_words.rearrange("c p b -> p c b"))
         nc.sync.dma_start(out=s_b[:], in_=s.rearrange("(g p t) -> p g t", p=P, t=4))
-        load_x(6)
-        load_x(7)
-        for i in range(4):
-            load_t(i)
+        nc.sync.dma_start(out=tg[0][:], in_=tg_view[0])
         nc.sync.dma_start(out=wt_b[:], in_=wt.rearrange("(g p t) -> p g t", p=P, t=4))
-        for i in range(4, 8):
-            load_t(i)
+        nc.sync.dma_start(out=tg[1][:], in_=tg_view[1])
         nc.gpsimd.tensor_copy(out=s_f[:], in_=s_b[:])
         nc.gpsimd.tensor_copy(out=wt_f[:], in_=wt_b[:])
 
@@ -285,20 +279,24 @@ def tile_lorafalogcoshgradient_w4_kernel(
 
         def run(eng, tok):
             kind = tok[0]
-            if kind == "X":
+            if kind in ("X", "Xa", "Xb"):
                 i = tok[1]
-                xw = xpool.tile([P, D], BF16, align_bytes=64, name="xw")
-                val["X", i] = xw
+                lo, hi = {"X": (0, D), "Xa": (0, 512), "Xb": (512, D)}[kind]
+                if ("X", i) not in val:
+                    xw = xpool.tile([P, D], BF16, align_bytes=64, name="xw")
+                    val["X", i] = xw
                 if eng == "V":
-                    nc.vector.tensor_copy(out=xw[:], in_=xb[i][:].bitcast(F8))
+                    nc.vector.tensor_copy(out=val["X", i][:, lo:hi], in_=xsrc[i][:, lo:hi].bitcast(F8))
                 else:
-                    nc.scalar.copy(out=xw[:], in_=xb[i][:].bitcast(F8))
-            elif kind == "T":
+                    nc.scalar.copy(out=val["X", i][:, lo:hi], in_=xsrc[i][:, lo:hi].bitcast(F8))
+            elif kind in ("T", "Ta"):
                 i = tok[1]
                 words = val["X", i][:].bitcast(F32)
-                bank = psums["T"].tile([P, 2, 2 * P], F32, name="t_bank")
-                val[tok] = bank
-                for c in range(2):
+                if kind == "Ta" or i > 0:
+                    bank = psums["T"].tile([P, 2, 2 * P], F32, name="t_bank")
+                    val["T", i] = bank
+                bank = val["T", i]
+                for c in (0,) if kind == "Ta" else (1,) if i == 0 else (0, 1):
                     for u in range(2):
                         nc.tensor.transpose(
                             bank[:, u, P * c : P * (c + 1)], words[:, 256 * c + u : 256 * (c + 1) : 2], ident[:]
@@ -332,7 +330,24 @@ def tile_lorafalogcoshgradient_w4_kernel(
                 )
             elif kind == "QU":
                 g = tok[1]
-                nc.vector.quantize_mx(out=u_codes[g][:].bitcast(F8X4), scales=u_sc[g][:], in_=ug_bf[g][:])
+                lo, hi = (0, R) if len(tok) == 2 else (256 * tok[2], 256 * (tok[2] + 1))
+                nc.vector.quantize_mx(
+                    out=u_codes[g][:, lo:hi].bitcast(F8X4), scales=u_sc[g][:, lo:hi], in_=ug_bf[g][:, 4 * lo : 4 * hi]
+                )
+            elif kind == "UA":
+                r = tok[1]
+                bank = psums["B"].tile([P, 4, P], F32, name="b_bank")
+                val[tok] = bank
+                for t in range(4):
+                    mm(bank[:, t, :], 4 + t, a_w, a_sc, P * r, P * (r + 1))
+            elif kind == "GA":
+                r = tok[1]
+                nc.vector.tensor_tensor(
+                    out=ug_bf[1][:, 512 * r : 512 * (r + 1)].rearrange("p (f t) -> p f t", t=4),
+                    in0=val["UA", r][:].rearrange("p t f -> p f t"),
+                    in1=s_f[:, 1, :].unsqueeze(1).to_broadcast([P, P, 4]),
+                    op=MULT,
+                )
             elif kind == "Y":
                 g, j = tok[1:]
                 bank = psums["Y"].tile([P, 4, P], F32, name="y_bank")
@@ -344,16 +359,20 @@ def tile_lorafalogcoshgradient_w4_kernel(
                 z = zs.tile([P, 512], F32, name="z")
                 val[tok] = z
                 nc.vector.tensor_tensor(
-                    out=z[:].rearrange("p (f t) -> p f t", t=4),
-                    in0=val["Y", g, j][:].rearrange("p t f -> p f t"),
-                    in1=tg[g][:, :, P * j : P * (j + 1)].rearrange("p t f -> p f t"),
+                    out=z[:].rearrange("p (t f) -> p t f", t=4),
+                    in0=val["Y", g, j][:],
+                    in1=tg[g][:, :, P * j : P * (j + 1)],
                     op=SUB,
                 )
             elif kind == "th":
                 g, j = tok[1:]
                 th = zs.tile([P, 512], F32, name="th")
                 val[tok] = th
-                nc.scalar.activation(out=th[:], in_=val["s", g, j][:], func=ACT.Tanh)
+                nc.scalar.activation(
+                    out=th[:].rearrange("p (c i t) -> p c t i", i=2, t=4),
+                    in_=val["s", g, j][:].rearrange("p (t c i) -> p c t i", t=4, i=2),
+                    func=ACT.Tanh,
+                )
             elif kind == "w":
                 g, j = tok[1:]
                 engine = nc.vector if eng == "V" else nc.gpsimd

@@ -3,10 +3,12 @@ from contextlib import ExitStack
 import concourse.mybir as mybir
 from concourse.masks import make_identity
 
-FLOPS = 2 * 1024 * 1024 * 512 * 2 + 2 * 1024 * 1024 * 1024
-
 P = 128
 D, F, R = 1024, 1024, 512
+TILES, BLOCKS = 8, 8
+
+FLOPS = 2 * 1024 * D * (R + F) + 2 * 1024 * R * F
+
 F32 = mybir.dt.float32
 BF16 = mybir.dt.bfloat16
 I32 = mybir.dt.int32
@@ -16,175 +18,37 @@ F8 = mybir.dt.float8_e4m3fn
 F8X4 = mybir.dt.float8_e4m3fn_x4
 F4X4 = mybir.dt.float4_e2m1fn_x4
 MULT = mybir.AluOpType.mult
-SUB = mybir.AluOpType.subtract
-ACT = mybir.ActivationFunctionType
-QE_SPAN = {(0, 0): 4, (0, 4): 4, (1, 0): 4, (1, 4): 2, (1, 6): 2}
-O_SPAN = {0: 4, 4: 2, 6: 2}
-O_POOL = {0: "TTBB", 4: "YYYY", 6: "TTBB"}
+SUBTRACT = mybir.AluOpType.subtract
+COPY = mybir.ActivationFunctionType.Copy
+TANH = mybir.ActivationFunctionType.Tanh
 
-ORDER = [
-    ("V", ("Xa", 0)),
-    ("S", ("Xb", 0)),
-    ("P", ("Ta", 0)),
-    ("S", ("X", 1)),
-    ("P", ("T", 0)),
-    ("V", ("M", 0)),
-    ("S", ("X", 2)),
-    ("P", ("T", 1)),
-    ("V", ("Q", 0)),
-    ("S", ("X", 3)),
-    ("V", ("M", 1)),
-    ("P", ("T", 2)),
-    ("S", ("X", 5)),
-    ("V", ("M", 2)),
-    ("P", ("T", 3)),
-    ("P", ("U", 0)),
-    ("S", ("X", 4)),
-    ("V", ("Q", 1)),
-    ("V", ("M", 3)),
-    ("P", ("U", 1)),
-    ("S", ("X", 7)),
-    ("P", ("T", 4)),
-    ("V", ("Q", 2)),
-    ("P", ("T", 5)),
-    ("V", ("Q", 3)),
-    ("S", ("G", 1)),
-    ("V", ("M", 4)),
-    ("P", ("Y", 0, 0)),
-    ("S", ("X", 6)),
-    ("P", ("Y", 0, 1)),
-    ("V", ("s", 0, 0)),
-    ("P", ("Y", 0, 2)),
-    ("V", ("Q", 4)),
-    ("S", ("th", 0, 0)),
-    ("P", ("Y", 0, 3)),
-    ("V", ("s", 0, 1)),
-    ("S", ("G", 0)),
-    ("P", ("Y", 0, 4)),
-    ("V", ("s", 0, 2)),
-    ("G", ("w", 0, 0)),
-    ("S", ("th", 0, 1)),
-    ("V", ("M", 5)),
-    ("P", ("U", 2)),
-    ("S", ("th", 0, 2)),
-    ("P", ("Y", 0, 5)),
-    ("G", ("w", 0, 1)),
-    ("V", ("s", 0, 3)),
-    ("S", ("G", 2)),
-    ("P", ("U", 3)),
-    ("V", ("s", 0, 5)),
-    ("P", ("T", 6)),
-    ("G", ("w", 0, 2)),
-    ("S", ("G", 3)),
-    ("V", ("s", 0, 4)),
-    ("P", ("Y", 0, 6)),
-    ("S", ("th", 0, 3)),
-    ("V", ("M", 6)),
-    ("P", ("T", 7)),
-    ("S", ("IU", 0, 0)),
-    ("G", ("w", 0, 3)),
-    ("P", ("U", 4)),
-    ("V", ("s", 0, 6)),
-    ("P", ("Y", 0, 7)),
-    ("V", ("M", 7)),
-    ("S", ("th", 0, 4)),
-    ("S", ("IU", 0, 1)),
-    ("V", ("Q", 6)),
-    ("V", ("Q", 5)),
-    ("V", ("Q", 7)),
-    ("S", ("th", 0, 5)),
-    ("P", ("U", 5)),
-    ("V", ("QE", 0, 0)),
-    ("P", ("Y", 1, 0)),
-    ("S", ("G", 4)),
-    ("V", ("QU", 0)),
-    ("P", ("Y", 1, 1)),
-    ("S", ("th", 0, 6)),
-    ("V", ("s", 0, 7)),
-    ("G", ("w", 0, 5)),
-    ("P", ("Y", 1, 2)),
-    ("S", ("G", 5)),
-    ("V", ("s", 1, 0)),
-    ("P", ("Y", 1, 3)),
-    ("S", ("th", 0, 7)),
-    ("G", ("w", 0, 4)),
-    ("V", ("s", 1, 1)),
-    ("P", ("Y", 1, 4)),
-    ("V", ("s", 1, 2)),
-    ("S", ("th", 1, 0)),
-    ("P", ("Y", 1, 5)),
-    ("G", ("w", 0, 7)),
-    ("V", ("s", 1, 3)),
-    ("S", ("th", 1, 2)),
-    ("P", ("U", 6)),
-    ("V", ("s", 1, 4)),
-    ("S", ("th", 1, 3)),
-    ("P", ("Y", 1, 6)),
-    ("G", ("w", 0, 6)),
-    ("V", ("s", 1, 5)),
-    ("P", ("Y", 1, 7)),
-    ("S", ("th", 1, 4)),
-    ("V", ("s", 1, 6)),
-    ("P", ("U", 7)),
-    ("S", ("th", 1, 1)),
-    ("V", ("s", 1, 7)),
-    ("P", ("O", 0, 0, 0)),
-    ("S", ("G", 6)),
-    ("P", ("O", 0, 1, 0)),
-    ("V", ("w", 1, 2)),
-    ("S", ("G", 7)),
-    ("V", ("w", 1, 0)),
-    ("P", ("O", 0, 2, 0)),
-    ("S", ("th", 1, 5)),
-    ("V", ("w", 1, 4)),
-    ("P", ("O", 0, 3, 0)),
-    ("V", ("w", 1, 1)),
-    ("S", ("IU", 1, 0)),
-    ("V", ("w", 1, 3)),
-    ("V", ("QE", 0, 4)),
-    ("S", ("th", 1, 6)),
-    ("V", ("w", 1, 5)),
-    ("S", ("IU", 1, 1)),
-    ("V", ("w", 1, 6)),
-    ("V", ("QE", 1, 0)),
-    ("S", ("th", 1, 7)),
-    ("V", ("QU", 1)),
-    ("V", ("QE", 1, 4)),
-    ("P", ("O", 0, 0, 1)),
-    ("V", ("w", 1, 7)),
-    ("P", ("O", 0, 1, 1)),
-    ("S", ("Oc", 0, 0)),
-    ("P", ("O", 0, 2, 1)),
-    ("V", ("Oc", 0, 1)),
-    ("P", ("O", 0, 3, 1)),
-    ("P", ("O", 4, 0, 0)),
-    ("S", ("Oc", 0, 2)),
-    ("P", ("O", 4, 1, 0)),
-    ("P", ("O", 4, 2, 0)),
-    ("V", ("Oc", 0, 3)),
-    ("P", ("O", 4, 3, 0)),
-    ("P", ("O", 4, 0, 1)),
-    ("P", ("O", 4, 1, 1)),
-    ("P", ("O", 4, 2, 1)),
-    ("V", ("QE", 1, 6)),
-    ("S", ("Oc", 4, 0)),
-    ("P", ("O", 4, 3, 1)),
-    ("P", ("O", 6, 0, 0)),
-    ("P", ("O", 6, 1, 0)),
-    ("S", ("Oc", 4, 2)),
-    ("V", ("Oc", 4, 3)),
-    ("P", ("O", 6, 2, 0)),
-    ("P", ("O", 6, 3, 0)),
-    ("P", ("O", 6, 0, 1)),
-    ("V", ("Oc", 4, 1)),
-    ("P", ("O", 6, 1, 1)),
-    ("P", ("O", 6, 2, 1)),
-    ("V", ("Oc", 6, 0)),
-    ("P", ("O", 6, 3, 1)),
-    ("S", ("Oc", 6, 1)),
-    ("V", ("Oc", 6, 2)),
-    ("S", ("Oc", 6, 3)),
-]
+VECTOR = """
+cast*2 scale*2 quant_x scale*2 quant_x*3 scale*2 minus quant_x minus quant_x minus*2 scale*2 minus
+quant_x*2 minus*5 quant_e quant_u minus*6 weigh*4 quant_e weigh quant_e quant_u weigh*3 quant_e
+leave*2 quant_e leave*4
+"""
+SCALAR = """
+cast*6 gate cast gate*2 tanh gate tanh*2 weave*2 tanh*2 gate*2 tanh*4 gate tanh gate tanh*2 weave
+tanh weave tanh*3 leave*6
+"""
+TENSOR = """
+turn*5 u turn*2 u y u y u y*2 turn*2 y*2 u y*2 u y*3 u*2 y*3 product y*2 product*23
+"""
+GPSIMD = """
+weigh*8
+"""
+
+E_RUNS = ((0, 0, 4), (0, 4, 4), (1, 0, 4), (1, 4, 2), (1, 6, 2))
+OUT_RUNS = ((0, 4), (4, 2), (6, 2))
+OUT_ORDER = ((0, 0), (1, 0), (0, 1), (1, 1), (2, 0), (2, 1))
+
+
+def expand(order):
+    names = []
+    for word in order.split():
+        parts = word.split("*")
+        names.extend([parts[0]] * (int(parts[1]) if len(parts) == 2 else 1))
+    return names
 
 
 def tile_lorafalogcoshgradient_w4_kernel(
@@ -193,235 +57,287 @@ def tile_lorafalogcoshgradient_w4_kernel(
     nc = tc.nc
     with ExitStack() as ctx:
         keep = ctx.enter_context(tc.tile_pool(name="keep", bufs=1))
-        xpool = ctx.enter_context(tc.tile_pool(name="xpool", bufs=8))
-        zs = ctx.enter_context(tc.tile_pool(name="zs", bufs=8))
-        outs = ctx.enter_context(tc.tile_pool(name="outs", bufs=8))
-        psums = {
-            "T": ctx.enter_context(tc.psum_pool(name="pt", bufs=2)),
-            "Y": ctx.enter_context(tc.psum_pool(name="py", bufs=4)),
-            "B": ctx.enter_context(tc.psum_pool(name="pb", bufs=2)),
-        }
+        x_pool = ctx.enter_context(tc.tile_pool(name="x_pool", bufs=TILES))
+        e_pool = ctx.enter_context(tc.tile_pool(name="e_pool", bufs=BLOCKS))
+        out_pool = ctx.enter_context(tc.tile_pool(name="out_pool", bufs=8))
+        turn_psum = ctx.enter_context(tc.psum_pool(name="turn_psum", bufs=2))
+        y_psum = ctx.enter_context(tc.psum_pool(name="y_psum", bufs=4))
+        u_psum = ctx.enter_context(tc.psum_pool(name="u_psum", bufs=2))
         ctx.enter_context(tc.manual_schedule())
 
-        warm = keep.tile([P, 1], F32)
-        nc.vector.memset(warm[:], 0.0)
-        nc.scalar.activation(out=warm[:], in_=warm[:], func=ACT.Tanh)
+        first = keep.tile([P, 1], F32)
+        nc.vector.memset(first[:], 0.0)
+        nc.scalar.activation(out=first[:], in_=first[:], func=TANH)
+
         wm_sc = keep.tile([P, 2, F], U8, align_bytes=64)
         a_sc = keep.tile([P, 2, R], U8, align_bytes=64)
         nc.vector.memset(wm_sc[:].rearrange("p c n -> p (c n)").bitcast(I32), 0)
         nc.vector.memset(a_sc[:].rearrange("p c n -> p (c n)").bitcast(I32), 0)
-        ident = keep.tile([P, P], F32)
-        make_identity(nc, ident[:])
+        identity = keep.tile([P, P], F32)
+        make_identity(nc, identity[:])
 
-        xb_view = x_bytes.rearrange("(g p t) k -> g p t k", p=P, t=4)
-        tg_view = target.rearrange("(g p t) f -> g p t f", p=P, t=4)
-        xb = [keep.tile([P, n, D], U8, align_bytes=64, name=f"xb{i}") for i, n in ((0, 1), (1, 1), (2, 2), (4, 2), (6, 2))]
-        tg = [keep.tile([P, 4, F], BF16, name=f"tg{i}") for i in range(2)]
-        xsp = keep.tile([P, 2, 4], F32)
+        byte_tiles = []
+        x_by = []
+        for first_tile, count in ((0, 1), (1, 1), (2, 2), (4, 2), (6, 2)):
+            held = keep.tile([P, count, D], U8, align_bytes=64, name=f"x_bytes_{first_tile}")
+            byte_tiles.append((held, first_tile, count))
+            x_by.extend([held[:, n, :] for n in range(count)])
+        x_rows = x_bytes.rearrange("(g p t) k -> g p t k", p=P, t=4)
+        target_rows = target.rearrange("(g p t) f -> g p t f", p=P, t=4)
+        x_sc = keep.tile([P, 2, 4], F32)
         wm_w = keep.tile([P, 2, 2 * F], U8, align_bytes=64)
         a_w = keep.tile([P, 2, 2 * R], U8, align_bytes=64)
-        s_b = keep.tile([P, 2, 4], BF16)
-        wt_b = keep.tile([P, 2, 4], BF16)
-        s_f = keep.tile([P, 2, 4], F32)
-        wt_f = keep.tile([P, 2, 4], F32)
+        targets = [keep.tile([P, 4, F], BF16, name=f"target_{g}") for g in range(2)]
+        s_bf = keep.tile([P, 2, 4], BF16)
+        wt_bf = keep.tile([P, 2, 4], BF16)
+        s_col = keep.tile([P, 2, 4], F32)
+        wt_col = keep.tile([P, 2, 4], F32)
 
-        xsrc = [xb[0][:, 0, :], xb[1][:, 0, :]] + [xb[1 + i // 2][:, i % 2, :] for i in range(2, 8)]
+        def load_bytes(held, tile, count):
+            nc.sync.dma_start(out=held[:], in_=x_rows[tile // 4, :, tile % 4 : tile % 4 + count, :])
 
-        def load_x(j, i, n):
-            nc.sync.dma_start(out=xb[j][:], in_=xb_view[i // 4, :, i % 4 : i % 4 + n, :])
-
-        def load_scales(dst, src):
+        def load_scales(planes, rows):
             for q in range(4):
                 nc.sync.dma_start(
-                    out=dst[32 * q : 32 * q + 4, :, :].bitcast(I32),
-                    in_=src[:, 4 * q : 4 * q + 4, :].rearrange("g q n -> q g n").bitcast(I32),
+                    out=planes[32 * q : 32 * q + 4, :, :].bitcast(I32),
+                    in_=rows[:, 4 * q : 4 * q + 4, :].rearrange("c q n -> q c n").bitcast(I32),
                 )
 
-        load_x(0, 0, 1)
-        load_x(1, 1, 1)
-        nc.sync.dma_start(out=xsp[:], in_=x_scale.rearrange("o (c p t) -> p (o c) t", p=P, t=4))
-        load_x(2, 2, 2)
+        load_bytes(*byte_tiles[0])
+        load_bytes(*byte_tiles[1])
+        nc.sync.dma_start(out=x_sc[:], in_=x_scale.rearrange("o (c p t) -> p (o c) t", p=P, t=4))
+        load_bytes(*byte_tiles[2])
         load_scales(wm_sc, wm_scales)
         nc.sync.dma_start(out=wm_w[:], in_=wm_words.rearrange("c p b -> p c b"))
-        load_x(3, 4, 2)
-        load_x(4, 6, 2)
+        load_bytes(*byte_tiles[3])
+        load_bytes(*byte_tiles[4])
         load_scales(a_sc, a_scales)
         nc.sync.dma_start(out=a_w[:], in_=a_words.rearrange("c p b -> p c b"))
-        nc.sync.dma_start(out=s_b[:], in_=s.rearrange("(g p t) -> p g t", p=P, t=4))
-        nc.sync.dma_start(out=tg[0][:], in_=tg_view[0])
-        nc.sync.dma_start(out=wt_b[:], in_=wt.rearrange("(g p t) -> p g t", p=P, t=4))
-        nc.sync.dma_start(out=tg[1][:], in_=tg_view[1])
-        nc.gpsimd.tensor_copy(out=s_f[:], in_=s_b[:])
-        nc.gpsimd.tensor_copy(out=wt_f[:], in_=wt_b[:])
+        nc.sync.dma_start(out=s_bf[:], in_=s.rearrange("(g p t) -> p g t", p=P, t=4))
+        nc.sync.dma_start(out=targets[0][:], in_=target_rows[0])
+        nc.sync.dma_start(out=wt_bf[:], in_=wt.rearrange("(g p t) -> p g t", p=P, t=4))
+        nc.sync.dma_start(out=targets[1][:], in_=target_rows[1])
+        nc.gpsimd.tensor_copy(out=s_col[:], in_=s_bf[:])
+        nc.gpsimd.tensor_copy(out=wt_col[:], in_=wt_bf[:])
 
-        x_codes = [keep.tile([P, 2 * P], U32, align_bytes=64, name=f"xc{i}") for i in range(8)]
-        x_sc = [keep.tile([P, 2 * P], U8, align_bytes=64, name=f"xsc{i}") for i in range(8)]
-        e_bf = [keep.tile([P, 4 * F], BF16, align_bytes=64, name=f"eb{i}") for i in range(2)]
-        e_codes = [keep.tile([P, F], U32, align_bytes=64, name=f"ec{i}") for i in range(2)]
-        e_sc = [keep.tile([P, F], U8, align_bytes=64, name=f"esc{i}") for i in range(2)]
-        ugp = [keep.tile([P, 4, R], BF16, name=f"up{i}") for i in range(2)]
-        ug_bf = [keep.tile([P, 4 * R], BF16, align_bytes=64, name=f"ub{i}") for i in range(2)]
-        u_codes = [keep.tile([P, R], U32, align_bytes=64, name=f"uc{i}") for i in range(2)]
-        u_sc = [keep.tile([P, R], U8, align_bytes=64, name=f"usc{i}") for i in range(2)]
-        val = {}
+        x_codes = [keep.tile([P, 2 * P], U32, align_bytes=64, name=f"x_codes_{i}") for i in range(TILES)]
+        x_planes = [keep.tile([P, 2 * P], U8, align_bytes=64, name=f"x_planes_{i}") for i in range(TILES)]
+        ug_flat = [keep.tile([P, 4, R], BF16, name=f"ug_flat_{g}") for g in range(2)]
+        ug_woven = [keep.tile([P, 4 * R], BF16, align_bytes=64, name=f"ug_woven_{g}") for g in range(2)]
+        ug_codes = [keep.tile([P, R], U32, align_bytes=64, name=f"ug_codes_{g}") for g in range(2)]
+        ug_planes = [keep.tile([P, R], U8, align_bytes=64, name=f"ug_planes_{g}") for g in range(2)]
+        e_woven = [keep.tile([P, 4 * F], BF16, align_bytes=64, name=f"e_woven_{g}") for g in range(2)]
+        e_codes = [keep.tile([P, F], U32, align_bytes=64, name=f"e_codes_{g}") for g in range(2)]
+        e_planes = [keep.tile([P, F], U8, align_bytes=64, name=f"e_planes_{g}") for g in range(2)]
+        made = {}
 
-        def mm(dst, i, words, scales, lo, hi):
+        def cast(copy, i, lo, hi):
+            if ("wide", i) not in made:
+                wide = x_pool.tile([P, D], BF16, align_bytes=64)
+                made["wide", i] = wide
+            copy(out=made["wide", i][:, lo:hi], in_=x_by[i][:, lo:hi].bitcast(F8))
+
+        def turn(i, passes):
+            words = made["wide", i][:].bitcast(F32)
+            if ("turned", i) not in made:
+                turned = turn_psum.tile([P, 2, 2 * P], F32, name="turn_bank")
+                made["turned", i] = turned
+            for c in passes:
+                for u in range(2):
+                    nc.tensor.transpose(
+                        made["turned", i][:, u, P * c : P * (c + 1)],
+                        words[:, 256 * c + u : 256 * (c + 1) : 2],
+                        identity[:],
+                    )
+
+        def scale(i):
+            scaled = x_pool.tile([P, D], BF16, align_bytes=64)
+            made["scaled", i] = scaled
+            nc.vector.tensor_tensor(
+                out=scaled[:].rearrange("p (c r u h) -> p c r u h", c=2, u=2, h=2),
+                in0=made["turned", i][:].bitcast(BF16).rearrange("p u (c r h) -> p c r u h", c=2, h=2),
+                in1=x_sc[:].rearrange("p c (u h) -> p c u h", u=2).unsqueeze(2).to_broadcast([P, 2, P, 2, 2]),
+                op=MULT,
+            )
+
+        def quant_x(i):
+            nc.vector.quantize_mx(
+                out=x_codes[i][:].bitcast(F8X4), scales=x_planes[i][:], in_=made["scaled", i][:]
+            )
+
+        def project(bank, i, words, planes, lo, hi):
             for c in range(2):
                 nc.tensor.matmul_mx(
-                    out=dst,
+                    out=bank,
                     lhsT=x_codes[i][:, P * c : P * (c + 1)].bitcast(F8X4),
-                    lhsT_scale=x_sc[i][:, P * c : P * (c + 1)],
+                    lhsT_scale=x_planes[i][:, P * c : P * (c + 1)],
                     rhs=words[:, c, 2 * lo : 2 * hi].bitcast(F4X4),
-                    rhs_scale=scales[:, c, lo:hi],
+                    rhs_scale=planes[:, c, lo:hi],
                     start=(c == 0),
                     stop=(c == 1),
                 )
 
-        def run(eng, tok):
-            kind = tok[0]
-            if kind in ("X", "Xa", "Xb"):
-                i = tok[1]
-                lo, hi = {"X": (0, D), "Xa": (0, 512), "Xb": (512, D)}[kind]
-                if ("X", i) not in val:
-                    xw = xpool.tile([P, D], BF16, align_bytes=64, name="xw")
-                    val["X", i] = xw
-                if eng == "V":
-                    nc.vector.tensor_copy(out=val["X", i][:, lo:hi], in_=xsrc[i][:, lo:hi].bitcast(F8))
-                else:
-                    nc.scalar.copy(out=val["X", i][:, lo:hi], in_=xsrc[i][:, lo:hi].bitcast(F8))
-            elif kind in ("T", "Ta"):
-                i = tok[1]
-                words = val["X", i][:].bitcast(F32)
-                if kind == "Ta" or i > 0:
-                    bank = psums["T"].tile([P, 2, 2 * P], F32, name="t_bank")
-                    val["T", i] = bank
-                bank = val["T", i]
-                for c in (0,) if kind == "Ta" else (1,) if i == 0 else (0, 1):
-                    for u in range(2):
-                        nc.tensor.transpose(
-                            bank[:, u, P * c : P * (c + 1)], words[:, 256 * c + u : 256 * (c + 1) : 2], ident[:]
-                        )
-            elif kind == "M":
-                i = tok[1]
-                xt = xpool.tile([P, D], BF16, align_bytes=64, name="xt")
-                val[tok] = xt
-                nc.vector.tensor_tensor(
-                    out=xt[:].rearrange("p (c r u e) -> p c r u e", c=2, u=2, e=2),
-                    in0=val["T", i][:].bitcast(BF16).rearrange("p u (c r e) -> p c r u e", c=2, e=2),
-                    in1=xsp[:].rearrange("p c (u e) -> p c u e", u=2).unsqueeze(2).to_broadcast([P, 2, P, 2, 2]),
-                    op=MULT,
-                )
-            elif kind == "Q":
-                i = tok[1]
-                nc.vector.quantize_mx(out=x_codes[i][:].bitcast(F8X4), scales=x_sc[i][:], in_=val["M", i][:])
-            elif kind == "U":
-                bank = psums["B"].tile([P, 512], F32, name="b_bank")
-                val[tok] = bank
-                mm(bank[:], tok[1], a_w, a_sc, 0, R)
-            elif kind == "G":
-                i = tok[1]
-                g, t = divmod(i, 4)
-                nc.scalar.activation(out=ugp[g][:, t, :], in_=val["U", i][:], func=ACT.Copy, scale=s_f[:, g, t : t + 1])
-            elif kind == "IU":
-                g, h = tok[1:]
-                nc.scalar.copy(
-                    out=ug_bf[g][:, 1024 * h : 1024 * (h + 1)].rearrange("p (c i t) -> p c t i", i=4, t=4),
-                    in_=ugp[g][:, :, 256 * h : 256 * (h + 1)].rearrange("p t (c i) -> p c t i", i=4),
-                )
-            elif kind == "QU":
-                g = tok[1]
-                lo, hi = (0, R) if len(tok) == 2 else (256 * tok[2], 256 * (tok[2] + 1))
-                nc.vector.quantize_mx(
-                    out=u_codes[g][:, lo:hi].bitcast(F8X4), scales=u_sc[g][:, lo:hi], in_=ug_bf[g][:, 4 * lo : 4 * hi]
-                )
-            elif kind == "UA":
-                r = tok[1]
-                bank = psums["B"].tile([P, 4, P], F32, name="b_bank")
-                val[tok] = bank
-                for t in range(4):
-                    mm(bank[:, t, :], 4 + t, a_w, a_sc, P * r, P * (r + 1))
-            elif kind == "GA":
-                r = tok[1]
-                nc.vector.tensor_tensor(
-                    out=ug_bf[1][:, 512 * r : 512 * (r + 1)].rearrange("p (f t) -> p f t", t=4),
-                    in0=val["UA", r][:].rearrange("p t f -> p f t"),
-                    in1=s_f[:, 1, :].unsqueeze(1).to_broadcast([P, P, 4]),
-                    op=MULT,
-                )
-            elif kind == "Y":
-                g, j = tok[1:]
-                bank = psums["Y"].tile([P, 4, P], F32, name="y_bank")
-                val[tok] = bank
-                for t in range(4):
-                    mm(bank[:, t, :], 4 * g + t, wm_w, wm_sc, P * j, P * (j + 1))
-            elif kind == "s":
-                g, j = tok[1:]
-                z = zs.tile([P, 512], F32, name="z")
-                val[tok] = z
-                nc.vector.tensor_tensor(
-                    out=z[:].rearrange("p (t f) -> p t f", t=4),
-                    in0=val["Y", g, j][:],
-                    in1=tg[g][:, :, P * j : P * (j + 1)],
-                    op=SUB,
-                )
-            elif kind == "th":
-                g, j = tok[1:]
-                th = zs.tile([P, 512], F32, name="th")
-                val[tok] = th
-                nc.scalar.activation(
-                    out=th[:].rearrange("p (c i t) -> p c t i", i=2, t=4),
-                    in_=val["s", g, j][:].rearrange("p (t c i) -> p c t i", t=4, i=2),
-                    func=ACT.Tanh,
-                )
-            elif kind == "w":
-                g, j = tok[1:]
-                engine = nc.vector if eng == "V" else nc.gpsimd
-                engine.tensor_tensor(
-                    out=e_bf[g][:, 512 * j : 512 * (j + 1)].rearrange("p (f t) -> p f t", t=4),
-                    in0=val["th", g, j][:].rearrange("p (f t) -> p f t", t=4),
-                    in1=wt_f[:, g, :].unsqueeze(1).to_broadcast([P, P, 4]),
-                    op=MULT,
-                )
-            elif kind == "QE":
-                g, j = tok[1:]
-                n = QE_SPAN[g, j]
-                nc.vector.quantize_mx(
-                    out=e_codes[g][:, P * j : P * (j + n)].bitcast(F8X4),
-                    scales=e_sc[g][:, P * j : P * (j + n)],
-                    in_=e_bf[g][:, 512 * j : 512 * (j + n)],
-                )
-            elif kind == "O":
-                j, rt, g = tok[1:]
-                n = P * O_SPAN[j]
-                if g == 0:
-                    tag = O_POOL[j][rt]
-                    if tag == "T":
-                        bank = psums["T"].tile([P, 512], F32, name="t_bank")
-                    elif tag == "B":
-                        bank = psums["B"].tile([P, 512], F32, name="b_bank")
-                    else:
-                        bank = psums["Y"].tile([P, 512], F32, name="y_bank")
-                    val["O", j, rt] = bank
-                nc.tensor.matmul_mx(
-                    out=val["O", j, rt][:, 0:n],
-                    lhsT=u_codes[g][:, P * rt : P * (rt + 1)].bitcast(F8X4),
-                    lhsT_scale=u_sc[g][:, P * rt : P * (rt + 1)],
-                    rhs=e_codes[g][:, P * j : P * j + n].bitcast(F8X4),
-                    rhs_scale=e_sc[g][:, P * j : P * j + n],
-                    start=(g == 0),
-                    stop=(g == 1),
-                )
-            elif kind == "Oc":
-                j, rt = tok[1:]
-                n = P * O_SPAN[j]
-                res = outs.tile([P, 512], F32, name="res")
-                if eng == "S":
-                    nc.scalar.activation(out=res[:, 0:n], in_=val["O", j, rt][:, 0:n], func=ACT.Copy, scale=1.0 / 32.0)
-                else:
-                    nc.vector.tensor_scalar(
-                        out=res[:, 0:n], in0=val["O", j, rt][:, 0:n], scalar1=1.0 / 32.0, scalar2=None, op0=MULT
-                    )
-                nc.sync.dma_start(out=out[P * rt : P * (rt + 1), P * j : P * j + n], in_=res[:, 0:n])
+        def u(i):
+            bank = u_psum.tile([P, R], F32, name="u_bank")
+            made["u", i] = bank
+            project(bank[:], i, a_w, a_sc, 0, R)
 
-        for eng, tok in ORDER:
-            run(eng, tok)
+        def gate(i):
+            g, t = divmod(i, 4)
+            nc.scalar.activation(
+                out=ug_flat[g][:, t, :], in_=made["u", i][:], func=COPY, scale=s_col[:, g, t : t + 1]
+            )
+
+        def weave(g, half):
+            nc.scalar.copy(
+                out=ug_woven[g][:, 1024 * half : 1024 * (half + 1)].rearrange("p (n m t) -> p n t m", m=4, t=4),
+                in_=ug_flat[g][:, :, 256 * half : 256 * (half + 1)].rearrange("p t (n m) -> p n t m", m=4),
+            )
+
+        def quant_u(g):
+            nc.vector.quantize_mx(out=ug_codes[g][:].bitcast(F8X4), scales=ug_planes[g][:], in_=ug_woven[g][:])
+
+        def y(g, j):
+            bank = y_psum.tile([P, 4, P], F32, name="y_bank")
+            made["y", g, j] = bank
+            for t in range(4):
+                project(bank[:, t, :], 4 * g + t, wm_w, wm_sc, P * j, P * (j + 1))
+
+        def minus(g, j):
+            loss_in = e_pool.tile([P, 4, P], F32)
+            made["minus", g, j] = loss_in
+            nc.vector.tensor_tensor(
+                out=loss_in[:], in0=made["y", g, j][:], in1=targets[g][:, :, P * j : P * (j + 1)], op=SUBTRACT
+            )
+
+        def tanh(g, j):
+            slope = e_pool.tile([P, P, 4], F32)
+            made["tanh", g, j] = slope
+            nc.scalar.activation(
+                out=slope[:].rearrange("p (n m) t -> p n t m", m=2),
+                in_=made["minus", g, j][:].rearrange("p t (n m) -> p n t m", m=2),
+                func=TANH,
+            )
+
+        def weigh(engine, g, j):
+            engine.tensor_tensor(
+                out=e_woven[g][:, 4 * P * j : 4 * P * (j + 1)].rearrange("p (f t) -> p f t", t=4),
+                in0=made["tanh", g, j][:],
+                in1=wt_col[:, g, :].unsqueeze(1).to_broadcast([P, P, 4]),
+                op=MULT,
+            )
+
+        def quant_e(g, j, count):
+            lo, hi = P * j, P * (j + count)
+            nc.vector.quantize_mx(
+                out=e_codes[g][:, lo:hi].bitcast(F8X4), scales=e_planes[g][:, lo:hi], in_=e_woven[g][:, 4 * lo : 4 * hi]
+            )
+
+        def product(run, g, rows):
+            j, count = OUT_RUNS[run]
+            lo, hi = P * j, P * (j + count)
+            if g == 0:
+                if run == 1:
+                    bank = y_psum.tile([P, R], F32, name="y_bank")
+                elif rows < 2:
+                    bank = turn_psum.tile([P, R], F32, name="turn_bank")
+                else:
+                    bank = u_psum.tile([P, R], F32, name="u_bank")
+                made["product", run, rows] = bank
+            nc.tensor.matmul_mx(
+                out=made["product", run, rows][:, 0 : hi - lo],
+                lhsT=ug_codes[g][:, P * rows : P * (rows + 1)].bitcast(F8X4),
+                lhsT_scale=ug_planes[g][:, P * rows : P * (rows + 1)],
+                rhs=e_codes[g][:, lo:hi].bitcast(F8X4),
+                rhs_scale=e_planes[g][:, lo:hi],
+                start=(g == 0),
+                stop=(g == 1),
+            )
+
+        def leave(engine, run, rows):
+            j, count = OUT_RUNS[run]
+            lo, hi = P * j, P * (j + count)
+            result = out_pool.tile([P, R], F32)
+            source = made["product", run, rows][:, 0 : hi - lo]
+            if engine == "scalar":
+                nc.scalar.activation(out=result[:, 0 : hi - lo], in_=source, func=COPY, scale=1.0 / 32.0)
+            else:
+                nc.vector.tensor_scalar(
+                    out=result[:, 0 : hi - lo], in0=source, scalar1=1.0 / 32.0, scalar2=None, op0=MULT
+                )
+            nc.sync.dma_start(out=out[P * rows : P * (rows + 1), lo:hi], in_=result[:, 0 : hi - lo])
+
+        steps = {}
+
+        def add(engine, kind, reads, writes, action):
+            steps.setdefault((engine, kind), []).append((reads, writes, action))
+
+        half = D // 2
+        add("vector", "cast", [], ("wide", 0, 0), lambda: cast(nc.vector.tensor_copy, 0, 0, half))
+        add("scalar", "cast", [], ("wide", 0, 1), lambda: cast(nc.scalar.copy, 0, half, D))
+        add("tensor", "turn", [("wide", 0, 0)], ("turned", 0, 0), lambda: turn(0, (0,)))
+        add("tensor", "turn", [("wide", 0, 1)], ("turned", 0), lambda: turn(0, (1,)))
+        add("vector", "cast", [], ("wide", 1), lambda: cast(nc.vector.tensor_copy, 1, 0, D))
+        for i in range(2, TILES):
+            add("scalar", "cast", [], ("wide", i), lambda i=i: cast(nc.scalar.copy, i, 0, D))
+        for i in range(1, TILES):
+            add("tensor", "turn", [("wide", i)], ("turned", i), lambda i=i: turn(i, (0, 1)))
+        for i in range(TILES):
+            add("vector", "scale", [("turned", i)], ("scaled", i), lambda i=i: scale(i))
+            add("vector", "quant_x", [("scaled", i)], ("x", i), lambda i=i: quant_x(i))
+            add("tensor", "u", [("x", i)], ("u", i), lambda i=i: u(i))
+            add("scalar", "gate", [("u", i)], ("gate", i), lambda i=i: gate(i))
+        for g in range(2):
+            tiles = range(4 * g, 4 * g + 4)
+            for n in range(2):
+                add("scalar", "weave", [("gate", i) for i in tiles], ("weave", g, n), lambda g=g, n=n: weave(g, n))
+            add("vector", "quant_u", [("weave", g, n) for n in range(2)], ("ug", g), lambda g=g: quant_u(g))
+            name, engine = (("gpsimd", nc.gpsimd), ("vector", nc.vector))[g]
+            for j in range(BLOCKS):
+                add("tensor", "y", [("x", i) for i in tiles], ("y", g, j), lambda g=g, j=j: y(g, j))
+                add("vector", "minus", [("y", g, j)], ("minus", g, j), lambda g=g, j=j: minus(g, j))
+                add("scalar", "tanh", [("minus", g, j)], ("tanh", g, j), lambda g=g, j=j: tanh(g, j))
+                add(
+                    name, "weigh", [("tanh", g, j)], ("weigh", g, j),
+                    lambda engine=engine, g=g, j=j: weigh(engine, g, j),
+                )
+        run_of = {}
+        for g, j, count in E_RUNS:
+            reads = [("weigh", g, b) for b in range(j, j + count)]
+            add("vector", "quant_e", reads, ("e", g, j), lambda g=g, j=j, count=count: quant_e(g, j, count))
+            for b in range(j, j + count):
+                run_of[g, b] = ("e", g, j)
+        for run, g in OUT_ORDER:
+            j, count = OUT_RUNS[run]
+            reads = [("ug", g)] + [run_of[g, b] for b in range(j, j + count)]
+            for rows in range(4):
+                add("tensor", "product", reads, ("product", run, g, rows), lambda run=run, g=g, rows=rows: product(run, g, rows))
+        for run in range(len(OUT_RUNS)):
+            for rows in range(4):
+                name = ("scalar", "vector")[(rows + (run == 2)) % 2]
+                add(
+                    name, "leave", [("product", run, 1, rows)], ("leave", run, rows),
+                    lambda name=name, run=run, rows=rows: leave(name, run, rows),
+                )
+
+        orders = {}
+        for engine, text in (("tensor", TENSOR), ("scalar", SCALAR), ("vector", VECTOR), ("gpsimd", GPSIMD)):
+            taken = {}
+            orders[engine] = []
+            for kind in expand(text):
+                number = taken.get(kind, 0)
+                taken[kind] = number + 1
+                orders[engine].append(steps[engine, kind][number])
+        written = set()
+        position = {engine: 0 for engine in orders}
+        total = sum(len(orders[engine]) for engine in orders)
+        assert total == sum(len(steps[key]) for key in steps)
+        for sweep in range(total):
+            for engine in orders:
+                if position[engine] < len(orders[engine]):
+                    reads, writes, action = orders[engine][position[engine]]
+                    if all(key in written for key in reads):
+                        action()
+                        written.add(writes)
+                        position[engine] = position[engine] + 1
+        assert len(written) == total

from contextlib import ExitStack

import concourse.mybir as mybir
from concourse.masks import make_identity

P = 128
D, F, R = 1024, 1024, 512
TILES, BLOCKS = 8, 8

FLOPS = 2 * 1024 * D * (R + F) + 2 * 1024 * R * F

F32 = mybir.dt.float32
BF16 = mybir.dt.bfloat16
I32 = mybir.dt.int32
U32 = mybir.dt.uint32
U8 = mybir.dt.uint8
F8 = mybir.dt.float8_e4m3fn
F8X4 = mybir.dt.float8_e4m3fn_x4
F4X4 = mybir.dt.float4_e2m1fn_x4
MULT = mybir.AluOpType.mult
SUBTRACT = mybir.AluOpType.subtract
COPY = mybir.ActivationFunctionType.Copy
TANH = mybir.ActivationFunctionType.Tanh

VECTOR = """
cast*2 scale*2 quant_x scale*2 quant_x*3 scale*2 minus quant_x minus quant_x minus*2 scale*2 minus
quant_x*2 minus*5 quant_e quant_u minus*6 weigh*4 quant_e weigh quant_e quant_u weigh*3 quant_e
leave*2 quant_e leave*4
"""
SCALAR = """
cast*6 gate cast gate*2 tanh gate tanh*2 weave*2 tanh*2 gate*2 tanh*4 gate tanh gate tanh*2 weave
tanh weave tanh*3 leave*6
"""
TENSOR = """
turn*5 u turn*2 u y u y u y*2 turn*2 y*2 u y*2 u y*3 u*2 y*3 product y*2 product*23
"""
GPSIMD = """
weigh*8
"""

E_RUNS = ((0, 0, 4), (0, 4, 4), (1, 0, 4), (1, 4, 2), (1, 6, 2))
OUT_RUNS = ((0, 4), (4, 2), (6, 2))
OUT_ORDER = ((0, 0), (1, 0), (0, 1), (1, 1), (2, 0), (2, 1))


def expand(order):
    names = []
    for word in order.split():
        parts = word.split("*")
        names.extend([parts[0]] * (int(parts[1]) if len(parts) == 2 else 1))
    return names


def tile_lorafalogcoshgradient_w4_kernel(
    tc, x_bytes, x_scale, wm_words, wm_scales, a_words, a_scales, target, s, wt, out
):
    nc = tc.nc
    with ExitStack() as ctx:
        keep = ctx.enter_context(tc.tile_pool(name="keep", bufs=1))
        x_pool = ctx.enter_context(tc.tile_pool(name="x_pool", bufs=TILES))
        e_pool = ctx.enter_context(tc.tile_pool(name="e_pool", bufs=BLOCKS))
        out_pool = ctx.enter_context(tc.tile_pool(name="out_pool", bufs=8))
        turn_psum = ctx.enter_context(tc.psum_pool(name="turn_psum", bufs=2))
        y_psum = ctx.enter_context(tc.psum_pool(name="y_psum", bufs=4))
        u_psum = ctx.enter_context(tc.psum_pool(name="u_psum", bufs=2))
        ctx.enter_context(tc.manual_schedule())

        first = keep.tile([P, 1], F32)
        nc.vector.memset(first[:], 0.0)
        nc.scalar.activation(out=first[:], in_=first[:], func=TANH)

        wm_sc = keep.tile([P, 2, F], U8, align_bytes=64)
        a_sc = keep.tile([P, 2, R], U8, align_bytes=64)
        nc.vector.memset(wm_sc[:].rearrange("p c n -> p (c n)").bitcast(I32), 0)
        nc.vector.memset(a_sc[:].rearrange("p c n -> p (c n)").bitcast(I32), 0)
        identity = keep.tile([P, P], F32)
        make_identity(nc, identity[:])

        byte_tiles = []
        x_by = []
        for first_tile, count in ((0, 1), (1, 1), (2, 2), (4, 2), (6, 2)):
            held = keep.tile([P, count, D], U8, align_bytes=64, name=f"x_bytes_{first_tile}")
            byte_tiles.append((held, first_tile, count))
            x_by.extend([held[:, n, :] for n in range(count)])
        x_rows = x_bytes.rearrange("(g p t) k -> g p t k", p=P, t=4)
        target_rows = target.rearrange("(g p t) f -> g p t f", p=P, t=4)
        x_sc = keep.tile([P, 2, 4], F32)
        wm_w = keep.tile([P, 2, 2 * F], U8, align_bytes=64)
        a_w = keep.tile([P, 2, 2 * R], U8, align_bytes=64)
        targets = [keep.tile([P, 4, F], BF16, name=f"target_{g}") for g in range(2)]
        s_bf = keep.tile([P, 2, 4], BF16)
        wt_bf = keep.tile([P, 2, 4], BF16)
        s_col = keep.tile([P, 2, 4], F32)
        wt_col = keep.tile([P, 2, 4], F32)

        def load_bytes(held, tile, count):
            nc.sync.dma_start(out=held[:], in_=x_rows[tile // 4, :, tile % 4 : tile % 4 + count, :])

        def load_scales(planes, rows):
            for q in range(4):
                nc.sync.dma_start(
                    out=planes[32 * q : 32 * q + 4, :, :].bitcast(I32),
                    in_=rows[:, 4 * q : 4 * q + 4, :].rearrange("c q n -> q c n").bitcast(I32),
                )

        load_bytes(*byte_tiles[0])
        load_bytes(*byte_tiles[1])
        nc.sync.dma_start(out=x_sc[:], in_=x_scale.rearrange("o (c p t) -> p (o c) t", p=P, t=4))
        load_bytes(*byte_tiles[2])
        load_scales(wm_sc, wm_scales)
        nc.sync.dma_start(out=wm_w[:], in_=wm_words.rearrange("c p b -> p c b"))
        load_bytes(*byte_tiles[3])
        load_bytes(*byte_tiles[4])
        load_scales(a_sc, a_scales)
        nc.sync.dma_start(out=a_w[:], in_=a_words.rearrange("c p b -> p c b"))
        nc.sync.dma_start(out=s_bf[:], in_=s.rearrange("(g p t) -> p g t", p=P, t=4))
        nc.sync.dma_start(out=targets[0][:], in_=target_rows[0])
        nc.sync.dma_start(out=wt_bf[:], in_=wt.rearrange("(g p t) -> p g t", p=P, t=4))
        nc.sync.dma_start(out=targets[1][:], in_=target_rows[1])
        nc.gpsimd.tensor_copy(out=s_col[:], in_=s_bf[:])
        nc.gpsimd.tensor_copy(out=wt_col[:], in_=wt_bf[:])

        x_codes = [keep.tile([P, 2 * P], U32, align_bytes=64, name=f"x_codes_{i}") for i in range(TILES)]
        x_planes = [keep.tile([P, 2 * P], U8, align_bytes=64, name=f"x_planes_{i}") for i in range(TILES)]
        ug_flat = [keep.tile([P, 4, R], BF16, name=f"ug_flat_{g}") for g in range(2)]
        ug_woven = [keep.tile([P, 4 * R], BF16, align_bytes=64, name=f"ug_woven_{g}") for g in range(2)]
        ug_codes = [keep.tile([P, R], U32, align_bytes=64, name=f"ug_codes_{g}") for g in range(2)]
        ug_planes = [keep.tile([P, R], U8, align_bytes=64, name=f"ug_planes_{g}") for g in range(2)]
        e_woven = [keep.tile([P, 4 * F], BF16, align_bytes=64, name=f"e_woven_{g}") for g in range(2)]
        e_codes = [keep.tile([P, F], U32, align_bytes=64, name=f"e_codes_{g}") for g in range(2)]
        e_planes = [keep.tile([P, F], U8, align_bytes=64, name=f"e_planes_{g}") for g in range(2)]
        made = {}

        def cast(copy, i, lo, hi):
            if ("wide", i) not in made:
                wide = x_pool.tile([P, D], BF16, align_bytes=64)
                made["wide", i] = wide
            copy(out=made["wide", i][:, lo:hi], in_=x_by[i][:, lo:hi].bitcast(F8))

        def turn(i, passes):
            words = made["wide", i][:].bitcast(F32)
            if ("turned", i) not in made:
                turned = turn_psum.tile([P, 2, 2 * P], F32, name="turn_bank")
                made["turned", i] = turned
            for c in passes:
                for u in range(2):
                    nc.tensor.transpose(
                        made["turned", i][:, u, P * c : P * (c + 1)],
                        words[:, 256 * c + u : 256 * (c + 1) : 2],
                        identity[:],
                    )

        def scale(i):
            scaled = x_pool.tile([P, D], BF16, align_bytes=64)
            made["scaled", i] = scaled
            nc.vector.tensor_tensor(
                out=scaled[:].rearrange("p (c r u h) -> p c r u h", c=2, u=2, h=2),
                in0=made["turned", i][:].bitcast(BF16).rearrange("p u (c r h) -> p c r u h", c=2, h=2),
                in1=x_sc[:].rearrange("p c (u h) -> p c u h", u=2).unsqueeze(2).to_broadcast([P, 2, P, 2, 2]),
                op=MULT,
            )

        def quant_x(i):
            nc.vector.quantize_mx(
                out=x_codes[i][:].bitcast(F8X4), scales=x_planes[i][:], in_=made["scaled", i][:]
            )

        def project(bank, i, words, planes, lo, hi):
            for c in range(2):
                nc.tensor.matmul_mx(
                    out=bank,
                    lhsT=x_codes[i][:, P * c : P * (c + 1)].bitcast(F8X4),
                    lhsT_scale=x_planes[i][:, P * c : P * (c + 1)],
                    rhs=words[:, c, 2 * lo : 2 * hi].bitcast(F4X4),
                    rhs_scale=planes[:, c, lo:hi],
                    start=(c == 0),
                    stop=(c == 1),
                )

        def u(i):
            bank = u_psum.tile([P, R], F32, name="u_bank")
            made["u", i] = bank
            project(bank[:], i, a_w, a_sc, 0, R)

        def gate(i):
            g, t = divmod(i, 4)
            nc.scalar.activation(
                out=ug_flat[g][:, t, :], in_=made["u", i][:], func=COPY, scale=s_col[:, g, t : t + 1]
            )

        def weave(g, half):
            nc.scalar.copy(
                out=ug_woven[g][:, 1024 * half : 1024 * (half + 1)].rearrange("p (n m t) -> p n t m", m=4, t=4),
                in_=ug_flat[g][:, :, 256 * half : 256 * (half + 1)].rearrange("p t (n m) -> p n t m", m=4),
            )

        def quant_u(g):
            nc.vector.quantize_mx(out=ug_codes[g][:].bitcast(F8X4), scales=ug_planes[g][:], in_=ug_woven[g][:])

        def y(g, j):
            bank = y_psum.tile([P, 4, P], F32, name="y_bank")
            made["y", g, j] = bank
            for t in range(4):
                project(bank[:, t, :], 4 * g + t, wm_w, wm_sc, P * j, P * (j + 1))

        def minus(g, j):
            loss_in = e_pool.tile([P, 4, P], F32)
            made["minus", g, j] = loss_in
            nc.vector.tensor_tensor(
                out=loss_in[:], in0=made["y", g, j][:], in1=targets[g][:, :, P * j : P * (j + 1)], op=SUBTRACT
            )

        def tanh(g, j):
            slope = e_pool.tile([P, P, 4], F32)
            made["tanh", g, j] = slope
            nc.scalar.activation(
                out=slope[:].rearrange("p (n m) t -> p n t m", m=2),
                in_=made["minus", g, j][:].rearrange("p t (n m) -> p n t m", m=2),
                func=TANH,
            )

        def weigh(engine, g, j):
            engine.tensor_tensor(
                out=e_woven[g][:, 4 * P * j : 4 * P * (j + 1)].rearrange("p (f t) -> p f t", t=4),
                in0=made["tanh", g, j][:],
                in1=wt_col[:, g, :].unsqueeze(1).to_broadcast([P, P, 4]),
                op=MULT,
            )

        def quant_e(g, j, count):
            lo, hi = P * j, P * (j + count)
            nc.vector.quantize_mx(
                out=e_codes[g][:, lo:hi].bitcast(F8X4), scales=e_planes[g][:, lo:hi], in_=e_woven[g][:, 4 * lo : 4 * hi]
            )

        def product(run, g, rows):
            j, count = OUT_RUNS[run]
            lo, hi = P * j, P * (j + count)
            if g == 0:
                if run == 1:
                    bank = y_psum.tile([P, R], F32, name="y_bank")
                elif rows < 2:
                    bank = turn_psum.tile([P, R], F32, name="turn_bank")
                else:
                    bank = u_psum.tile([P, R], F32, name="u_bank")
                made["product", run, rows] = bank
            nc.tensor.matmul_mx(
                out=made["product", run, rows][:, 0 : hi - lo],
                lhsT=ug_codes[g][:, P * rows : P * (rows + 1)].bitcast(F8X4),
                lhsT_scale=ug_planes[g][:, P * rows : P * (rows + 1)],
                rhs=e_codes[g][:, lo:hi].bitcast(F8X4),
                rhs_scale=e_planes[g][:, lo:hi],
                start=(g == 0),
                stop=(g == 1),
            )

        def leave(engine, run, rows):
            j, count = OUT_RUNS[run]
            lo, hi = P * j, P * (j + count)
            result = out_pool.tile([P, R], F32)
            source = made["product", run, rows][:, 0 : hi - lo]
            if engine == "scalar":
                nc.scalar.activation(out=result[:, 0 : hi - lo], in_=source, func=COPY, scale=1.0 / 32.0)
            else:
                nc.vector.tensor_scalar(
                    out=result[:, 0 : hi - lo], in0=source, scalar1=1.0 / 32.0, scalar2=None, op0=MULT
                )
            nc.sync.dma_start(out=out[P * rows : P * (rows + 1), lo:hi], in_=result[:, 0 : hi - lo])

        steps = {}

        def add(engine, kind, reads, writes, action):
            steps.setdefault((engine, kind), []).append((reads, writes, action))

        half = D // 2
        add("vector", "cast", [], ("wide", 0, 0), lambda: cast(nc.vector.tensor_copy, 0, 0, half))
        add("scalar", "cast", [], ("wide", 0, 1), lambda: cast(nc.scalar.copy, 0, half, D))
        add("tensor", "turn", [("wide", 0, 0)], ("turned", 0, 0), lambda: turn(0, (0,)))
        add("tensor", "turn", [("wide", 0, 1)], ("turned", 0), lambda: turn(0, (1,)))
        add("vector", "cast", [], ("wide", 1), lambda: cast(nc.vector.tensor_copy, 1, 0, D))
        for i in range(2, TILES):
            add("scalar", "cast", [], ("wide", i), lambda i=i: cast(nc.scalar.copy, i, 0, D))
        for i in range(1, TILES):
            add("tensor", "turn", [("wide", i)], ("turned", i), lambda i=i: turn(i, (0, 1)))
        for i in range(TILES):
            add("vector", "scale", [("turned", i)], ("scaled", i), lambda i=i: scale(i))
            add("vector", "quant_x", [("scaled", i)], ("x", i), lambda i=i: quant_x(i))
            add("tensor", "u", [("x", i)], ("u", i), lambda i=i: u(i))
            add("scalar", "gate", [("u", i)], ("gate", i), lambda i=i: gate(i))
        for g in range(2):
            tiles = range(4 * g, 4 * g + 4)
            for n in range(2):
                add("scalar", "weave", [("gate", i) for i in tiles], ("weave", g, n), lambda g=g, n=n: weave(g, n))
            add("vector", "quant_u", [("weave", g, n) for n in range(2)], ("ug", g), lambda g=g: quant_u(g))
            name, engine = (("gpsimd", nc.gpsimd), ("vector", nc.vector))[g]
            for j in range(BLOCKS):
                add("tensor", "y", [("x", i) for i in tiles], ("y", g, j), lambda g=g, j=j: y(g, j))
                add("vector", "minus", [("y", g, j)], ("minus", g, j), lambda g=g, j=j: minus(g, j))
                add("scalar", "tanh", [("minus", g, j)], ("tanh", g, j), lambda g=g, j=j: tanh(g, j))
                add(
                    name, "weigh", [("tanh", g, j)], ("weigh", g, j),
                    lambda engine=engine, g=g, j=j: weigh(engine, g, j),
                )
        run_of = {}
        for g, j, count in E_RUNS:
            reads = [("weigh", g, b) for b in range(j, j + count)]
            add("vector", "quant_e", reads, ("e", g, j), lambda g=g, j=j, count=count: quant_e(g, j, count))
            for b in range(j, j + count):
                run_of[g, b] = ("e", g, j)
        for run, g in OUT_ORDER:
            j, count = OUT_RUNS[run]
            reads = [("ug", g)] + [run_of[g, b] for b in range(j, j + count)]
            for rows in range(4):
                add("tensor", "product", reads, ("product", run, g, rows), lambda run=run, g=g, rows=rows: product(run, g, rows))
        for run in range(len(OUT_RUNS)):
            for rows in range(4):
                name = ("scalar", "vector")[(rows + (run == 2)) % 2]
                add(
                    name, "leave", [("product", run, 1, rows)], ("leave", run, rows),
                    lambda name=name, run=run, rows=rows: leave(name, run, rows),
                )

        orders = {}
        for engine, text in (("tensor", TENSOR), ("scalar", SCALAR), ("vector", VECTOR), ("gpsimd", GPSIMD)):
            taken = {}
            orders[engine] = []
            for kind in expand(text):
                number = taken.get(kind, 0)
                taken[kind] = number + 1
                orders[engine].append(steps[engine, kind][number])
        written = set()
        position = {engine: 0 for engine in orders}
        total = sum(len(orders[engine]) for engine in orders)
        assert total == sum(len(steps[key]) for key in steps)
        for sweep in range(total):
            for engine in orders:
                if position[engine] < len(orders[engine]):
                    reads, writes, action = orders[engine][position[engine]]
                    if all(key in written for key in reads):
                        action()
                        written.add(writes)
                        position[engine] = position[engine] + 1
        assert len(written) == total
